import numpy as np
import ml_dtypes


def mxq(x, axis, fmt="e4m3"):
    dtype, down = {"e4m3": (ml_dtypes.float8_e4m3fn, 7), "e5m2": (ml_dtypes.float8_e5m2, 14)}[fmt]
    v = np.moveaxis(np.asarray(x, np.float32).astype(ml_dtypes.bfloat16).astype(np.float64), axis, -1)
    blocks = v.reshape(v.shape[:-1] + (-1, 32))
    amax = np.abs(blocks).max(-1, keepdims=True)
    byte = np.maximum(np.where(amax > 0, np.frexp(amax)[1] - 1 + 127, 0) - down, 1)
    scale = np.exp2(byte - 127.0)
    codes = (blocks / scale).astype(np.float32).astype(dtype).astype(np.float64)
    return np.moveaxis((codes * scale).reshape(v.shape), -1, axis)


WIDE = False


def mx_kscale(k):
    if not WIDE:
        return np.ones(k)
    levels = np.array([30, -30])
    if k % 512:
        return np.exp2(np.random.permutation(np.resize(levels, k // 32))).repeat(32)
    a = np.empty((k // 512, 16))
    for p in range(k // 512):
        a[p, :8] = np.random.permutation(np.resize(levels, 8))
        for g in range(8):
            far = levels[np.abs(levels - a[p, g]) >= 10]
            a[p, g + 8] = far[np.random.randint(len(far))]
    return np.exp2(a.ravel()).repeat(32)


def f64(x):
    return np.asarray(x).astype(np.float64)


def striped(idx):
    return np.tile(idx.reshape(-1, 16).T, (8, 1)).astype(np.uint16)


def unstriped(offs):
    return offs[:16].T.reshape(-1).astype(np.int64)


E2M1 = np.array([0.0, 0.5, 1.0, 1.5, 2.0, 3.0, 4.0, 6.0, -0.0, -0.5, -1.0, -1.5, -2.0, -3.0, -4.0, -6.0])


def pack_weight(w, fmt):
    k, n = w.shape
    w = f64(np.asarray(w, np.float32).astype(ml_dtypes.bfloat16)).reshape(k // 32, 32, n)
    amax = np.abs(w).max(1)
    if fmt == "e4m3":
        byte = np.frexp(amax)[1] - 1 + 127 - 7
    else:
        mant, ex = np.frexp(amax / 6.0)
        byte = np.where(mant > 0.5, ex, ex - 1) + 127
    byte = np.clip(np.where(amax > 0, byte, 1), 1, 254)
    scaled = (w * np.exp2(127.0 - byte)[:, None, :]).reshape(k, n).astype(np.float32)
    by_word = np.ascontiguousarray(scaled.reshape(k // 512, 128, 4, n).transpose(0, 1, 3, 2))
    if fmt == "e4m3":
        words = by_word.astype(ml_dtypes.float8_e4m3fn).view(np.uint8)
    else:
        c = by_word.astype(ml_dtypes.float4_e2m1fn).view(np.uint8) & 0xF
        words = (c[..., 0::2] | (c[..., 1::2] << 4)).reshape(k // 512, 128, 2 * n)
    return np.ascontiguousarray(words), np.ascontiguousarray(byte.astype(np.uint8).reshape(k // 512, 16, n))


def unpack_weight(words, scales, fmt):
    g, _, n = scales.shape
    words = np.ascontiguousarray(words).reshape(g, 128, n, -1)
    if fmt == "e4m3":
        vals = words.view(ml_dtypes.float8_e4m3fn).astype(np.float64)
    else:
        nib = np.empty((g, 128, n, 4), np.uint8)
        nib[..., 0::2] = words & 0xF
        nib[..., 1::2] = words >> 4
        vals = E2M1[nib]
    vals = vals * np.repeat(np.exp2(scales.astype(np.float64) - 127.0), 8, axis=1)[..., None]
    return vals.transpose(0, 1, 3, 2).reshape(g * 512, n)


def relu(v):
    return np.maximum(v, 0.0)


def d_relu(v):
    return (v > 0).astype(np.float64)


K, T, E, C, H, N = 256, 2048, 4, 512, 512, 512


def by_expert(wq, xq):
    return np.concatenate([wq[e].T @ xq[:, e * C:(e + 1) * C] for e in range(E)], axis=1)


def setup_inputs():
    n = np.random.standard_normal
    s = mx_kscale(N)[:, None]
    u = mx_kscale(H)
    w2 = [pack_weight(m, "e2m1") for m in n((E, N, H)) / np.sqrt(N) / s[None] * u[None, None, :]]
    w1 = [pack_weight(m, "e2m1") for m in n((E, H, K)) / np.sqrt(H) / u[None, :, None]]
    w3 = [pack_weight(m, "e2m1") for m in n((E, H, K)) / np.sqrt(H) / u[None, :, None]]
    return {
        "dyT": (n((N, T)) * s).astype(np.float32),
        "a1": n((H, E * C)).astype(np.float32),
        "a3": n((H, E * C)).astype(np.float32),
        "w2_words": np.stack([m[0] for m in w2]),
        "w2_scales": np.stack([m[1] for m in w2]),
        "w1_words": np.stack([m[0] for m in w1]),
        "w1_scales": np.stack([m[1] for m in w1]),
        "w3_words": np.stack([m[0] for m in w3]),
        "w3_scales": np.stack([m[1] for m in w3]),
        "gate": np.tile(np.random.uniform(0.2, 1.0, E * C), (N, 1)).astype(np.float32),
        "offs": striped(np.random.permutation(T)[:E * C]),
    }


def reference(dyT, a1, a3, w2_words, w2_scales, w1_words, w1_scales, w3_words, w3_scales, gate, offs):
    idx = unstriped(offs)
    w2 = np.stack([unpack_weight(w2_words[e], w2_scales[e], "e2m1") for e in range(E)])
    w1 = np.stack([unpack_weight(w1_words[e], w1_scales[e], "e2m1") for e in range(E)])
    w3 = np.stack([unpack_weight(w3_words[e], w3_scales[e], "e2m1") for e in range(E)])
    gq = mxq(f64(gate) * f64(dyT)[:, idx], 0, "e5m2")
    dh = by_expert(w2, gq)
    da1 = dh * f64(a3) * d_relu(f64(a1))
    da3 = dh * relu(f64(a1))
    dx = by_expert(w1, mxq(da1, 0, "e5m2")) + by_expert(w3, mxq(da3, 0, "e5m2"))
    out = np.zeros((K, T))
    out[:, idx] = dx
    return out

@@ -1,0 +1,230 @@
+from contextlib import ExitStack
+
+import concourse.mybir as mybir
+
+K, T, E, C, H, N = 256, 2048, 4, 512, 512, 512
+
+P = 128
+PACK = 4
+K_BLOCKS = K // P
+LIST_ROWS = 16
+RUN = 4
+
+FLOPS = 2 * E * C * (N * H + 2 * H * K)
+WEIGHTS = E * (N * H + 2 * H * K)
+BYTES = 4 * (N * T + 2 * H * E * C + E * C + K * T) + WEIGHTS // 2 + WEIGHTS // 32 + 2 * P * (E * C // LIST_ROWS)
+
+F32 = mybir.dt.float32
+BF16 = mybir.dt.bfloat16
+I32 = mybir.dt.int32
+U32 = mybir.dt.uint32
+U16 = mybir.dt.uint16
+U8 = mybir.dt.uint8
+E5M2X4 = mybir.dt.float8_e5m2_x4
+E2M1X4 = mybir.dt.float4_e2m1fn_x4
+MULT = mybir.AluOpType.mult
+COPY = mybir.ActivationFunctionType.Copy
+RELU = mybir.ActivationFunctionType.Relu
+SIGN = mybir.ActivationFunctionType.Sign
+
+
+def tile_moe_bdx_glu_relu_kernel(
+    tc, dyT, a1, a3, w2_words, w2_scales, w1_words, w1_scales, w3_words, w3_scales, gate, offs, out
+):
+    nc = tc.nc
+    with ExitStack() as ctx:
+        held = ctx.enter_context(tc.tile_pool(name="held", bufs=1))
+        token_wide = ctx.enter_context(tc.tile_pool(name="token_wide", bufs=PACK))
+        gathered = ctx.enter_context(tc.tile_pool(name="gathered", bufs=E))
+        ring = ctx.enter_context(tc.tile_pool(name="ring", bufs=2))
+        saved = ctx.enter_context(tc.tile_pool(name="saved", bufs=3))
+        dh_banks = ctx.enter_context(tc.psum_pool(name="dh_banks", bufs=6))
+        dx_banks = ctx.enter_context(tc.psum_pool(name="dx_banks", bufs=2))
+
+        def slots(e):
+            return slice(e * C, (e + 1) * C)
+
+        offsets = held.tile([P, E * C // LIST_ROWS], U16, name="offsets")
+        nc.sync.dma_start(offsets[:], offs)
+
+        def entries(e):
+            return offsets[:, e * C // LIST_ROWS : (e + 1) * C // LIST_ROWS]
+
+        def load_words(tile, dram):
+            nc.sync.dma_start(tile[:].bitcast(I32), dram.rearrange("e s p b -> p (e s) b").bitcast(I32))
+
+        def load_scales(tile, dram):
+            for q in range(4):
+                nc.sync.dma_start(
+                    tile[32 * q : 32 * q + 4].bitcast(I32),
+                    dram[:, 0, 4 * q : 4 * q + 4, :].rearrange("e f i -> f e i").bitcast(I32),
+                )
+
+        w2_arrived = held.tile([P, E, 2 * H], U8, name="w2_arrived", align_bytes=64)
+        w2_arrived_scale = held.tile([P, E, H], U8, name="w2_arrived_scale", align_bytes=64)
+        w2_code = held.tile([P, E, 2 * H], U8, name="w2_code", align_bytes=64)
+        w2_scale = held.tile([P, E, H], U8, name="w2_scale", align_bytes=64)
+        w1_code = held.tile([P, E, 2 * K], U8, name="w1_code", align_bytes=64)
+        w1_scale = held.tile([P, E, K], U8, name="w1_scale", align_bytes=64)
+        w3_code = held.tile([P, E, 2 * K], U8, name="w3_code", align_bytes=64)
+        w3_scale = held.tile([P, E, K], U8, name="w3_scale", align_bytes=64)
+        for tile in (w2_arrived_scale, w1_scale, w3_scale):
+            nc.gpsimd.memset(tile[:].bitcast(I32), 0)
+
+        gates = held.tile([P, E * C], F32, name="gates")
+        dy_planes = {}
+        a1_saved, a3_saved = {}, {}
+
+        def load_gates(first, last):
+            columns = slice(first * C, (last + 1) * C)
+            nc.sync.dma_start(gates[:, columns], gate[0:P, columns])
+
+        def load_plane(j):
+            dy_planes[j] = token_wide.tile([P, T], F32, name="token_wide_tile")
+            nc.sync.dma_start(dy_planes[j][:], dyT.rearrange("(p j) s -> p j s", j=PACK)[:, j, :])
+
+        def load_saved(tiles, dram, e, name):
+            tiles[e] = saved.tile([P, PACK, C], F32, name=name)
+            nc.sync.dma_start(tiles[e][:], dram.rearrange("(p t) s -> p t s", t=PACK)[:, :, slots(e)])
+
+        def load_a1(e):
+            load_saved(a1_saved, a1, e, "a1_saved")
+
+        def load_a3(e):
+            load_saved(a3_saved, a3, e, "a3_saved")
+
+        load_words(w2_arrived, w2_words)
+        load_scales(w2_arrived_scale, w2_scales)
+        load_gates(0, 0)
+        load_plane(0)
+        load_gates(1, 1)
+        for j in range(1, PACK):
+            load_plane(j)
+        load_a1(0)
+        load_a3(0)
+        load_gates(2, 3)
+        load_a1(1)
+        load_a3(1)
+        load_words(w1_code, w1_words)
+        load_words(w3_code, w3_words)
+        load_scales(w1_scale, w1_scales)
+        load_scales(w3_scale, w3_scales)
+        load_a1(2)
+        load_a3(2)
+
+        nc.vector.tensor_copy(
+            w2_code[:].bitcast(U16).rearrange("p e (t m) -> p e t m", t=PACK),
+            w2_arrived[:].bitcast(U16).rearrange("p e (m t) -> p e t m", t=PACK),
+        )
+        nc.vector.tensor_copy(
+            w2_scale[:].rearrange("p e (t m) -> p e t m", t=PACK),
+            w2_arrived_scale[:].rearrange("p e (m t) -> p e t m", t=PACK),
+        )
+
+        def from_rows(ap):
+            return ap.rearrange("p t (c i) -> p c t i", i=RUN)
+
+        def to_columns(ap):
+            return ap.rearrange("p (c i) t -> p c t i", i=RUN)
+
+        def quantise(values, name):
+            code = ring.tile([P, C], U32, name=name + "_code", align_bytes=64)
+            scale = ring.tile([P, C], U8, name=name + "_scale", align_bytes=64)
+            nc.vector.quantize_mx(
+                out=code[:].bitcast(E5M2X4), scales=scale[:], in_=values.rearrange("p c t -> p (c t)")
+            )
+            return code, scale
+
+        gradients, gradient_codes, zero_one, da1_rounded, da3_rounded, dx = {}, {}, {}, {}, {}, {}
+
+        def gather(e):
+            gradients[e] = gathered.tile([P, PACK, C], F32, name="gradients_tile")
+            for j in range(PACK):
+                nc.vector.tensor_tensor(
+                    gradients[e][:, j, :], dy_planes[j][:].indirect(entries(e)), gates[:, slots(e)], MULT
+                )
+
+        def apply_relu(e):
+            nc.scalar.activation(a1_saved[e][:], a1_saved[e][:], RELU)
+            zero_one[e] = ring.tile([P, C, PACK], BF16, name="zero_one_tile")
+            nc.scalar.activation(to_columns(zero_one[e][:]), from_rows(a1_saved[e][:]), SIGN)
+
+        def quantise_gradients(e):
+            rounded = ring.tile([P, C, PACK], BF16, name="g_rounded", align_bytes=64)
+            nc.scalar.activation(to_columns(rounded[:]), from_rows(gradients[e][:]), COPY)
+            gradient_codes[e] = quantise(rounded[:], "g")
+
+        def hidden_gradients(e):
+            code, scale = gradient_codes[e]
+            dh = ring.tile([P, PACK, C], F32, name="dh")
+            for t in range(PACK):
+                bank = dh_banks.tile([P, C], F32, name="dh_bank")
+                nc.tensor.matmul_mx(
+                    out=bank[:],
+                    lhsT=w2_code[:, e, 2 * P * t : 2 * P * (t + 1)].bitcast(E2M1X4),
+                    lhsT_scale=w2_scale[:, e, P * t : P * (t + 1)],
+                    rhs=code[:].bitcast(E5M2X4),
+                    rhs_scale=scale[:],
+                    start=True,
+                    stop=True,
+                )
+                nc.scalar.copy(dh[:, t, :], bank[:])
+            da1_rounded[e] = ring.tile([P, C, PACK], BF16, name="da1_rounded", align_bytes=64)
+            da3_rounded[e] = ring.tile([P, C, PACK], BF16, name="da3_rounded", align_bytes=64)
+            for rounded, factor in ((da1_rounded[e], a3_saved[e]), (da3_rounded[e], a1_saved[e])):
+                nc.vector.tensor_tensor(to_columns(rounded[:]), from_rows(factor[:]), from_rows(dh[:]), MULT)
+
+        def output_gradients(e):
+            nc.vector.tensor_tensor(da1_rounded[e][:], da1_rounded[e][:], zero_one[e][:], MULT)
+            da3_code, da3_scale = quantise(da3_rounded[e][:], "da3")
+            da1_code, da1_scale = quantise(da1_rounded[e][:], "da1")
+            for k in range(K_BLOCKS):
+                bank = dx_banks.tile([P, C], F32, name="dx_bank")
+                for w_code, w_scale, code, scale, first in (
+                    (w3_code, w3_scale, da3_code, da3_scale, True),
+                    (w1_code, w1_scale, da1_code, da1_scale, False),
+                ):
+                    nc.tensor.matmul_mx(
+                        out=bank[:],
+                        lhsT=w_code[:, e, 2 * P * k : 2 * P * (k + 1)].bitcast(E2M1X4),
+                        lhsT_scale=w_scale[:, e, P * k : P * (k + 1)],
+                        rhs=code[:].bitcast(E5M2X4),
+                        rhs_scale=scale[:],
+                        start=first,
+                        stop=not first,
+                    )
+                dx[e, k] = held.tile([P, C], F32, name=f"dx_{e}_{k}")
+                nc.scalar.copy(dx[e, k][:], bank[:])
+
+        windows = {}
+
+        def scatter(e, k):
+            if k not in windows:
+                windows[k] = token_wide.tile([P, T], F32, name="token_wide_tile")
+            nc.vector.tensor_copy(windows[k][:].indirect(entries(e)), dx[e, k][:])
+
+        def expert(e):
+            apply_relu(e)
+            quantise_gradients(e)
+            hidden_gradients(e)
+            output_gradients(e)
+
+        gather(0)
+        gather(1)
+        expert(0)
+        load_a1(3)
+        load_a3(3)
+        expert(1)
+        scatter(0, 0)
+        scatter(0, 1)
+        gather(2)
+        gather(3)
+        expert(2)
+        scatter(1, 0)
+        scatter(1, 1)
+        expert(3)
+        scatter(2, 0)
+        scatter(2, 1)
+        for k in range(K_BLOCKS):
+            scatter(3, k)
+            nc.sync.dma_start(out[k * P : (k + 1) * P, :], windows[k][:])

@@ -1,12 +1,14 @@
 from contextlib import ExitStack
 
 import concourse.mybir as mybir
+from concourse.masks import make_identity
 
 K, T, E, C, H, N = 256, 2048, 4, 512, 512, 512
 
 P = 128
 PACK = 4
 K_BLOCKS = K // P
+SLOT_BLOCKS = C // P
 LIST_ROWS = 16
 RUN = 4
 
@@ -35,11 +37,12 @@ def tile_moe_bdx_glu_relu_kernel(
     with ExitStack() as ctx:
         held = ctx.enter_context(tc.tile_pool(name="held", bufs=1))
         token_wide = ctx.enter_context(tc.tile_pool(name="token_wide", bufs=PACK))
-        gathered = ctx.enter_context(tc.tile_pool(name="gathered", bufs=E))
+        gathered = ctx.enter_context(tc.tile_pool(name="gathered", bufs=3))
         ring = ctx.enter_context(tc.tile_pool(name="ring", bufs=2))
         saved = ctx.enter_context(tc.tile_pool(name="saved", bufs=3))
+        by_slot_runs = ctx.enter_context(tc.tile_pool(name="by_slot_runs", bufs=8))
+        mx_banks = ctx.enter_context(tc.psum_pool(name="mx_banks", bufs=1))
         dh_banks = ctx.enter_context(tc.psum_pool(name="dh_banks", bufs=6))
-        dx_banks = ctx.enter_context(tc.psum_pool(name="dx_banks", bufs=2))
 
         def slots(e):
             return slice(e * C, (e + 1) * C)
@@ -60,16 +63,16 @@ def tile_moe_bdx_glu_relu_kernel(
                     dram[:, 0, 4 * q : 4 * q + 4, :].rearrange("e f i -> f e i").bitcast(I32),
                 )
 
-        w2_arrived = held.tile([P, E, 2 * H], U8, name="w2_arrived", align_bytes=64)
-        w2_arrived_scale = held.tile([P, E, H], U8, name="w2_arrived_scale", align_bytes=64)
         w2_code = held.tile([P, E, 2 * H], U8, name="w2_code", align_bytes=64)
         w2_scale = held.tile([P, E, H], U8, name="w2_scale", align_bytes=64)
         w1_code = held.tile([P, E, 2 * K], U8, name="w1_code", align_bytes=64)
         w1_scale = held.tile([P, E, K], U8, name="w1_scale", align_bytes=64)
         w3_code = held.tile([P, E, 2 * K], U8, name="w3_code", align_bytes=64)
         w3_scale = held.tile([P, E, K], U8, name="w3_scale", align_bytes=64)
-        for tile in (w2_arrived_scale, w1_scale, w3_scale):
+        for tile in (w2_scale, w1_scale, w3_scale):
             nc.gpsimd.memset(tile[:].bitcast(I32), 0)
+        identity = held.tile([P, P], F32, name="identity")
+        make_identity(nc, identity[:])
 
         gates = held.tile([P, E * C], F32, name="gates")
         dy_planes = {}
@@ -93,33 +96,24 @@ def tile_moe_bdx_glu_relu_kernel(
         def load_a3(e):
             load_saved(a3_saved, a3, e, "a3_saved")
 
-        load_words(w2_arrived, w2_words)
-        load_scales(w2_arrived_scale, w2_scales)
         load_gates(0, 0)
         load_plane(0)
         load_gates(1, 1)
         for j in range(1, PACK):
             load_plane(j)
+        load_gates(2, 3)
+        load_words(w2_code, w2_words)
+        load_scales(w2_scale, w2_scales)
         load_a1(0)
         load_a3(0)
-        load_gates(2, 3)
         load_a1(1)
-        load_a3(1)
         load_words(w1_code, w1_words)
         load_words(w3_code, w3_words)
         load_scales(w1_scale, w1_scales)
         load_scales(w3_scale, w3_scales)
+        load_a3(1)
         load_a1(2)
         load_a3(2)
-
-        nc.vector.tensor_copy(
-            w2_code[:].bitcast(U16).rearrange("p e (t m) -> p e t m", t=PACK),
-            w2_arrived[:].bitcast(U16).rearrange("p e (m t) -> p e t m", t=PACK),
-        )
-        nc.vector.tensor_copy(
-            w2_scale[:].rearrange("p e (t m) -> p e t m", t=PACK),
-            w2_arrived_scale[:].rearrange("p e (m t) -> p e t m", t=PACK),
-        )
 
         def from_rows(ap):
             return ap.rearrange("p t (c i) -> p c t i", i=RUN)
@@ -135,7 +129,11 @@ def tile_moe_bdx_glu_relu_kernel(
             )
             return code, scale
 
+        mx_bank = [mx_banks.tile([P, C], F32, name=f"mx_bank_{n}") for n in range(2)]
+
         gradients, gradient_codes, zero_one, da1_rounded, da3_rounded, dx = {}, {}, {}, {}, {}, {}
+
+        da1_codes, da3_codes = {}, {}
 
         def gather(e):
             gradients[e] = gathered.tile([P, PACK, C], F32, name="gradients_tile")
@@ -146,6 +144,8 @@ def tile_moe_bdx_glu_relu_kernel(
 
         def apply_relu(e):
             nc.scalar.activation(a1_saved[e][:], a1_saved[e][:], RELU)
+
+        def relu_slope(e):
             zero_one[e] = ring.tile([P, C, PACK], BF16, name="zero_one_tile")
             nc.scalar.activation(to_columns(zero_one[e][:]), from_rows(a1_saved[e][:]), SIGN)
 
@@ -156,30 +156,40 @@ def tile_moe_bdx_glu_relu_kernel(
 
         def hidden_gradients(e):
             code, scale = gradient_codes[e]
-            dh = ring.tile([P, PACK, C], F32, name="dh")
-            for t in range(PACK):
-                bank = dh_banks.tile([P, C], F32, name="dh_bank")
+            da1_rounded[e] = ring.tile([P, C, PACK], BF16, name="da1_rounded", align_bytes=64)
+            da3_rounded[e] = ring.tile([P, C, PACK], BF16, name="da3_rounded", align_bytes=64)
+            for b in range(SLOT_BLOCKS):
+                block = slice(P * b, P * (b + 1))
+                by_slot = mx_bank[b % 2]
                 nc.tensor.matmul_mx(
-                    out=bank[:],
-                    lhsT=w2_code[:, e, 2 * P * t : 2 * P * (t + 1)].bitcast(E2M1X4),
-                    lhsT_scale=w2_scale[:, e, P * t : P * (t + 1)],
-                    rhs=code[:].bitcast(E5M2X4),
-                    rhs_scale=scale[:],
+                    out=by_slot[:],
+                    lhsT=code[:, block].bitcast(E5M2X4),
+                    lhsT_scale=scale[:, block],
+                    rhs=w2_code[:, e, :].bitcast(E2M1X4),
+                    rhs_scale=w2_scale[:, e, :],
                     start=True,
                     stop=True,
                 )
-                nc.scalar.copy(dh[:, t, :], bank[:])
-            da1_rounded[e] = ring.tile([P, C, PACK], BF16, name="da1_rounded", align_bytes=64)
-            da3_rounded[e] = ring.tile([P, C, PACK], BF16, name="da3_rounded", align_bytes=64)
-            for rounded, factor in ((da1_rounded[e], a3_saved[e]), (da3_rounded[e], a1_saved[e])):
-                nc.vector.tensor_tensor(to_columns(rounded[:]), from_rows(factor[:]), from_rows(dh[:]), MULT)
+                runs = by_slot_runs.tile([P, PACK, P], F32, name="runs")
+                nc.scalar.copy(runs[:], by_slot[:].rearrange("p (m t) -> p t m", t=PACK))
+                dh = dh_banks.tile([P, PACK, P], F32, name="dh")
+                for t in range(PACK):
+                    nc.tensor.transpose(dh[:, t, :], runs[:, t, :], identity[:])
+                for rounded, factor in ((da1_rounded[e], a3_saved[e]), (da3_rounded[e], a1_saved[e])):
+                    nc.vector.tensor_tensor(
+                        to_columns(rounded[:, block, :]), from_rows(dh[:]), from_rows(factor[:, :, block]), MULT
+                    )
+
+        def quantise_hidden_gradients(e):
+            nc.vector.tensor_tensor(da1_rounded[e][:], da1_rounded[e][:], zero_one[e][:], MULT)
+            da3_codes[e] = quantise(da3_rounded[e][:], "da3")
+            da1_codes[e] = quantise(da1_rounded[e][:], "da1")
 
         def output_gradients(e):
-            nc.vector.tensor_tensor(da1_rounded[e][:], da1_rounded[e][:], zero_one[e][:], MULT)
-            da3_code, da3_scale = quantise(da3_rounded[e][:], "da3")
-            da1_code, da1_scale = quantise(da1_rounded[e][:], "da1")
+            da3_code, da3_scale = da3_codes[e]
+            da1_code, da1_scale = da1_codes[e]
             for k in range(K_BLOCKS):
-                bank = dx_banks.tile([P, C], F32, name="dx_bank")
+                bank = mx_bank[k]
                 for w_code, w_scale, code, scale, first in (
                     (w3_code, w3_scale, da3_code, da3_scale, True),
                     (w1_code, w1_scale, da1_code, da1_scale, False),
@@ -203,28 +213,29 @@ def tile_moe_bdx_glu_relu_kernel(
                 windows[k] = token_wide.tile([P, T], F32, name="token_wide_tile")
             nc.vector.tensor_copy(windows[k][:].indirect(entries(e)), dx[e, k][:])
 
-        def expert(e):
-            apply_relu(e)
-            quantise_gradients(e)
-            hidden_gradients(e)
-            output_gradients(e)
-
         gather(0)
         gather(1)
-        expert(0)
-        load_a1(3)
-        load_a3(3)
-        expert(1)
-        scatter(0, 0)
-        scatter(0, 1)
+        quantise_gradients(0)
         gather(2)
         gather(3)
-        expert(2)
-        scatter(1, 0)
-        scatter(1, 1)
-        expert(3)
-        scatter(2, 0)
-        scatter(2, 1)
+        quantise_gradients(1)
+        for e in range(E):
+            apply_relu(e)
+            hidden_gradients(e)
+            if e == 0:
+                load_a1(3)
+                load_a3(3)
+            else:
+                output_gradients(e - 1)
+            relu_slope(e)
+            if e + 2 < E:
+                quantise_gradients(e + 2)
+            if e > 0:
+                scatter(e - 1, 0)
+            quantise_hidden_gradients(e)
+            if e > 0:
+                scatter(e - 1, 1)
+        output_gradients(E - 1)
         for k in range(K_BLOCKS):
-            scatter(3, k)
+            scatter(E - 1, k)
             nc.sync.dma_start(out[k * P : (k + 1) * P, :], windows[k][:])

@@ -99,12 +99,14 @@ def tile_moe_bdx_glu_relu_kernel(
         load_gates(0, 0)
         load_plane(0)
         load_gates(1, 1)
-        for j in range(1, PACK):
-            load_plane(j)
-        load_gates(2, 3)
+        load_plane(1)
+        load_plane(2)
+        load_gates(2, 2)
+        load_a1(0)
+        load_plane(3)
+        load_gates(3, 3)
         load_words(w2_code, w2_words)
         load_scales(w2_scale, w2_scales)
-        load_a1(0)
         load_a3(0)
         load_a1(1)
         load_words(w1_code, w1_words)
@@ -131,9 +133,12 @@ def tile_moe_bdx_glu_relu_kernel(
 
         mx_bank = [mx_banks.tile([P, C], F32, name=f"mx_bank_{n}") for n in range(2)]
 
-        gradients, gradient_codes, zero_one, da1_rounded, da3_rounded, dx = {}, {}, {}, {}, {}, {}
+        gradients, gradient_codes, zero_one, dx = {}, {}, {}, {}
 
-        da1_codes, da3_codes = {}, {}
+        da1_codes, da3_codes, a1_first, a3_first = {}, {}, {}, {}
+
+        da1_tile = held.tile([P, C, PACK], BF16, name="da1_tile", align_bytes=64)
+        da3_tile = held.tile([P, C, PACK], BF16, name="da3_tile", align_bytes=64)
 
         def gather(e):
             gradients[e] = gathered.tile([P, PACK, C], F32, name="gradients_tile")
@@ -143,21 +148,27 @@ def tile_moe_bdx_glu_relu_kernel(
                 )
 
         def apply_relu(e):
-            nc.scalar.activation(a1_saved[e][:], a1_saved[e][:], RELU)
+            nc.scalar.activation(a1_saved[e][:, :, P:], a1_saved[e][:, :, P:], RELU)
+            a1_first[e] = ring.tile([P, P, PACK], F32, name="a1_first_tile")
+            a3_first[e] = ring.tile([P, P, PACK], F32, name="a3_first_tile")
+            nc.scalar.activation(to_columns(a1_first[e][:]), from_rows(a1_saved[e][:, :, 0:P]), RELU)
+            nc.scalar.activation(to_columns(a3_first[e][:]), from_rows(a3_saved[e][:, :, 0:P]), COPY)
 
         def relu_slope(e):
             zero_one[e] = ring.tile([P, C, PACK], BF16, name="zero_one_tile")
-            nc.scalar.activation(to_columns(zero_one[e][:]), from_rows(a1_saved[e][:]), SIGN)
+            nc.scalar.activation(zero_one[e][:, 0:P, :], a1_first[e][:], SIGN)
+            nc.scalar.activation(to_columns(zero_one[e][:, P:, :]), from_rows(a1_saved[e][:, :, P:]), SIGN)
 
         def quantise_gradients(e):
-            rounded = ring.tile([P, C, PACK], BF16, name="g_rounded", align_bytes=64)
+            if e == 1:
+                rounded = da3_tile
+            else:
+                rounded = ring.tile([P, C, PACK], BF16, name="g_rounded", align_bytes=64)
             nc.scalar.activation(to_columns(rounded[:]), from_rows(gradients[e][:]), COPY)
             gradient_codes[e] = quantise(rounded[:], "g")
 
         def hidden_gradients(e):
             code, scale = gradient_codes[e]
-            da1_rounded[e] = ring.tile([P, C, PACK], BF16, name="da1_rounded", align_bytes=64)
-            da3_rounded[e] = ring.tile([P, C, PACK], BF16, name="da3_rounded", align_bytes=64)
             for b in range(SLOT_BLOCKS):
                 block = slice(P * b, P * (b + 1))
                 by_slot = mx_bank[b % 2]
@@ -175,15 +186,21 @@ def tile_moe_bdx_glu_relu_kernel(
                 dh = dh_banks.tile([P, PACK, P], F32, name="dh")
                 for t in range(PACK):
                     nc.tensor.transpose(dh[:, t, :], runs[:, t, :], identity[:])
-                for rounded, factor in ((da1_rounded[e], a3_saved[e]), (da3_rounded[e], a1_saved[e])):
+                if b == 0:
+                    dh_first = ring.tile([P, P, PACK], F32, name="dh_first")
+                    nc.scalar.copy(dh_first[:], dh[:].rearrange("p t c -> p c t"))
+                    nc.gpsimd.tensor_tensor(da3_tile[:, block, :], dh_first[:], a1_first[e][:], MULT)
+                    nc.gpsimd.tensor_tensor(da1_tile[:, block, :], dh_first[:], a3_first[e][:], MULT)
+                    continue
+                for rounded, factor in ((da3_tile, a1_saved[e]), (da1_tile, a3_saved[e])):
                     nc.vector.tensor_tensor(
                         to_columns(rounded[:, block, :]), from_rows(dh[:]), from_rows(factor[:, :, block]), MULT
                     )
 
         def quantise_hidden_gradients(e):
-            nc.vector.tensor_tensor(da1_rounded[e][:], da1_rounded[e][:], zero_one[e][:], MULT)
-            da3_codes[e] = quantise(da3_rounded[e][:], "da3")
-            da1_codes[e] = quantise(da1_rounded[e][:], "da1")
+            nc.vector.tensor_tensor(da1_tile[:], da1_tile[:], zero_one[e][:], MULT)
+            da3_codes[e] = quantise(da3_tile[:], "da3")
+            da1_codes[e] = quantise(da1_tile[:], "da1")
 
         def output_gradients(e):
             da3_code, da3_scale = da3_codes[e]
@@ -227,14 +244,15 @@ def tile_moe_bdx_glu_relu_kernel(
                 load_a3(3)
             else:
                 output_gradients(e - 1)
+            if 0 < e < E - 1:
+                quantise_gradients(e + 1)
             relu_slope(e)
-            if e + 2 < E:
-                quantise_gradients(e + 2)
             if e > 0:
                 scatter(e - 1, 0)
-            quantise_hidden_gradients(e)
-            if e > 0:
+            if 0 < e < E - 1:
                 scatter(e - 1, 1)
+            quantise_hidden_gradients(e)
+        scatter(E - 2, 1)
         output_gradients(E - 1)
         for k in range(K_BLOCKS):
             scatter(E - 1, k)

@@ -12,6 +12,8 @@ SLOT_BLOCKS = C // P
 LIST_ROWS = 16
 RUN = 4
 
+HALVES = (slice(0, C // 2), slice(C // 2, C))
+
 FLOPS = 2 * E * C * (N * H + 2 * H * K)
 WEIGHTS = E * (N * H + 2 * H * K)
 BYTES = 4 * (N * T + 2 * H * E * C + E * C + K * T) + WEIGHTS // 2 + WEIGHTS // 32 + 2 * P * (E * C // LIST_ROWS)
@@ -37,12 +39,13 @@ def tile_moe_bdx_glu_relu_kernel(
     with ExitStack() as ctx:
         held = ctx.enter_context(tc.tile_pool(name="held", bufs=1))
         token_wide = ctx.enter_context(tc.tile_pool(name="token_wide", bufs=PACK))
-        gathered = ctx.enter_context(tc.tile_pool(name="gathered", bufs=3))
+        in_turn = ctx.enter_context(tc.tile_pool(name="in_turn", bufs=1))
         ring = ctx.enter_context(tc.tile_pool(name="ring", bufs=2))
         saved = ctx.enter_context(tc.tile_pool(name="saved", bufs=3))
         by_slot_runs = ctx.enter_context(tc.tile_pool(name="by_slot_runs", bufs=8))
         mx_banks = ctx.enter_context(tc.psum_pool(name="mx_banks", bufs=1))
-        dh_banks = ctx.enter_context(tc.psum_pool(name="dh_banks", bufs=6))
+        first_bank = ctx.enter_context(tc.psum_pool(name="first_bank", bufs=1))
+        dh_banks = ctx.enter_context(tc.psum_pool(name="dh_banks", bufs=SLOT_BLOCKS - 1))
 
         def slots(e):
             return slice(e * C, (e + 1) * C)
@@ -87,7 +90,7 @@ def tile_moe_bdx_glu_relu_kernel(
             nc.sync.dma_start(dy_planes[j][:], dyT.rearrange("(p j) s -> p j s", j=PACK)[:, j, :])
 
         def load_saved(tiles, dram, e, name):
-            tiles[e] = saved.tile([P, PACK, C], F32, name=name)
+            tiles[e] = saved.tile([P, PACK, C], F32, name=name, align_bytes=64)
             nc.sync.dma_start(tiles[e][:], dram.rearrange("(p t) s -> p t s", t=PACK)[:, :, slots(e)])
 
         def load_a1(e):
@@ -109,11 +112,11 @@ def tile_moe_bdx_glu_relu_kernel(
         load_scales(w2_scale, w2_scales)
         load_a3(0)
         load_a1(1)
+        load_a3(1)
         load_words(w1_code, w1_words)
         load_words(w3_code, w3_words)
         load_scales(w1_scale, w1_scales)
         load_scales(w3_scale, w3_scales)
-        load_a3(1)
         load_a1(2)
         load_a3(2)
 
@@ -123,55 +126,64 @@ def tile_moe_bdx_glu_relu_kernel(
         def to_columns(ap):
             return ap.rearrange("p (c i) t -> p c t i", i=RUN)
 
-        def quantise(values, name):
-            code = ring.tile([P, C], U32, name=name + "_code", align_bytes=64)
+        def quantise(values, name, pool):
+            code = pool.tile([P, C], U32, name=name + "_code", align_bytes=64)
             scale = ring.tile([P, C], U8, name=name + "_scale", align_bytes=64)
             nc.vector.quantize_mx(
                 out=code[:].bitcast(E5M2X4), scales=scale[:], in_=values.rearrange("p c t -> p (c t)")
             )
             return code, scale
 
-        mx_bank = [mx_banks.tile([P, C], F32, name=f"mx_bank_{n}") for n in range(2)]
+        mx_bank = [mx_banks.tile([P, C], F32, name=f"mx_bank_{n}") for n in range(SLOT_BLOCKS)]
 
-        gradients, gradient_codes, zero_one, dx = {}, {}, {}, {}
+        def mx_bank_of(e, b):
+            return mx_bank[b if e % 2 == 0 else SLOT_BLOCKS - 1 - b]
 
-        da1_codes, da3_codes, a1_first, a3_first = {}, {}, {}, {}
+        first_and_last = held.tile([P, PACK + 1, C], F32, name="first_and_last")
+        gradients = {0: first_and_last[:, 1:, :], E - 1: first_and_last[:, :PACK, :]}
+        for e in range(1, E - 1):
+            gradients[e] = held.tile([P, PACK, C], F32, name=f"gradients_{e}")[:]
+        gradient_codes, zero_one, dx = {}, {}, {}
+
+        da1_codes, da3_codes, relu_a1, a3_first = {}, {}, {}, {}
 
         da1_tile = held.tile([P, C, PACK], BF16, name="da1_tile", align_bytes=64)
         da3_tile = held.tile([P, C, PACK], BF16, name="da3_tile", align_bytes=64)
 
         def gather(e):
-            gradients[e] = gathered.tile([P, PACK, C], F32, name="gradients_tile")
             for j in range(PACK):
                 nc.vector.tensor_tensor(
                     gradients[e][:, j, :], dy_planes[j][:].indirect(entries(e)), gates[:, slots(e)], MULT
                 )
 
         def apply_relu(e):
-            nc.scalar.activation(a1_saved[e][:, :, P:], a1_saved[e][:, :, P:], RELU)
-            a1_first[e] = ring.tile([P, P, PACK], F32, name="a1_first_tile")
+            relu_a1[e] = ring.tile([P, C, PACK], F32, name="relu_a1_tile")
             a3_first[e] = ring.tile([P, P, PACK], F32, name="a3_first_tile")
-            nc.scalar.activation(to_columns(a1_first[e][:]), from_rows(a1_saved[e][:, :, 0:P]), RELU)
+            for half in HALVES:
+                nc.scalar.activation(to_columns(relu_a1[e][:, half, :]), from_rows(a1_saved[e][:, :, half]), RELU)
             nc.scalar.activation(to_columns(a3_first[e][:]), from_rows(a3_saved[e][:, :, 0:P]), COPY)
 
         def relu_slope(e):
             zero_one[e] = ring.tile([P, C, PACK], BF16, name="zero_one_tile")
-            nc.scalar.activation(zero_one[e][:, 0:P, :], a1_first[e][:], SIGN)
-            nc.scalar.activation(to_columns(zero_one[e][:, P:, :]), from_rows(a1_saved[e][:, :, P:]), SIGN)
+            for half in HALVES:
+                nc.scalar.activation(zero_one[e][:, half, :], relu_a1[e][:, half, :], SIGN)
 
         def quantise_gradients(e):
             if e == 1:
-                rounded = da3_tile
+                rounded = da1_tile[:]
+            elif e == 0:
+                rounded = da3_tile[:]
             else:
-                rounded = ring.tile([P, C, PACK], BF16, name="g_rounded", align_bytes=64)
-            nc.scalar.activation(to_columns(rounded[:]), from_rows(gradients[e][:]), COPY)
-            gradient_codes[e] = quantise(rounded[:], "g")
+                rows = a3_saved[e - 2][:, 0:2, :].rearrange("p t c -> p (t c)")
+                rounded = rows.bitcast(BF16).rearrange("p (c t) -> p c t", t=PACK)
+            nc.scalar.activation(to_columns(rounded), from_rows(gradients[e]), COPY)
+            gradient_codes[e] = quantise(rounded, "g", ring)
 
         def hidden_gradients(e):
             code, scale = gradient_codes[e]
             for b in range(SLOT_BLOCKS):
                 block = slice(P * b, P * (b + 1))
-                by_slot = mx_bank[b % 2]
+                by_slot = mx_bank_of(e, b)
                 nc.tensor.matmul_mx(
                     out=by_slot[:],
                     lhsT=code[:, block].bitcast(E5M2X4),
@@ -183,77 +195,92 @@ def tile_moe_bdx_glu_relu_kernel(
                 )
                 runs = by_slot_runs.tile([P, PACK, P], F32, name="runs")
                 nc.scalar.copy(runs[:], by_slot[:].rearrange("p (m t) -> p t m", t=PACK))
-                dh = dh_banks.tile([P, PACK, P], F32, name="dh")
+                dh = (dh_banks if b else first_bank).tile([P, PACK, P], F32, name="dh")
                 for t in range(PACK):
                     nc.tensor.transpose(dh[:, t, :], runs[:, t, :], identity[:])
                 if b == 0:
                     dh_first = ring.tile([P, P, PACK], F32, name="dh_first")
                     nc.scalar.copy(dh_first[:], dh[:].rearrange("p t c -> p c t"))
-                    nc.gpsimd.tensor_tensor(da3_tile[:, block, :], dh_first[:], a1_first[e][:], MULT)
                     nc.gpsimd.tensor_tensor(da1_tile[:, block, :], dh_first[:], a3_first[e][:], MULT)
+                    nc.gpsimd.tensor_tensor(da3_tile[:, block, :], dh_first[:], relu_a1[e][:, block, :], MULT)
                     continue
-                for rounded, factor in ((da3_tile, a1_saved[e]), (da1_tile, a3_saved[e])):
-                    nc.vector.tensor_tensor(
-                        to_columns(rounded[:, block, :]), from_rows(dh[:]), from_rows(factor[:, :, block]), MULT
-                    )
+                nc.vector.tensor_tensor(
+                    da3_tile[:, block, :], dh[:].rearrange("p t c -> p c t"), relu_a1[e][:, block, :], MULT
+                )
+                nc.vector.tensor_tensor(
+                    to_columns(da1_tile[:, block, :]), from_rows(dh[:]), from_rows(a3_saved[e][:, :, block]), MULT
+                )
 
         def quantise_hidden_gradients(e):
             nc.vector.tensor_tensor(da1_tile[:], da1_tile[:], zero_one[e][:], MULT)
-            da3_codes[e] = quantise(da3_tile[:], "da3")
-            da1_codes[e] = quantise(da1_tile[:], "da1")
+            da3_codes[e] = quantise(da3_tile[:], "da3", ring)
+            da1_codes[e] = quantise(da1_tile[:], "da1", in_turn if e < E - 1 else ring)
 
-        def output_gradients(e):
-            da3_code, da3_scale = da3_codes[e]
-            da1_code, da1_scale = da1_codes[e]
-            for k in range(K_BLOCKS):
-                bank = mx_bank[k]
-                for w_code, w_scale, code, scale, first in (
-                    (w3_code, w3_scale, da3_code, da3_scale, True),
-                    (w1_code, w1_scale, da1_code, da1_scale, False),
-                ):
-                    nc.tensor.matmul_mx(
-                        out=bank[:],
-                        lhsT=w_code[:, e, 2 * P * k : 2 * P * (k + 1)].bitcast(E2M1X4),
-                        lhsT_scale=w_scale[:, e, P * k : P * (k + 1)],
-                        rhs=code[:].bitcast(E5M2X4),
-                        rhs_scale=scale[:],
-                        start=first,
-                        stop=not first,
-                    )
-                dx[e, k] = held.tile([P, C], F32, name=f"dx_{e}_{k}")
-                nc.scalar.copy(dx[e, k][:], bank[:])
+        def output_gradients(e, k, tile):
+            bank = mx_bank_of(min(e + 1, E - 1), SLOT_BLOCKS - K_BLOCKS + k)
+            for w_code, w_scale, (code, scale), first in (
+                (w3_code, w3_scale, da3_codes[e], True),
+                (w1_code, w1_scale, da1_codes[e], False),
+            ):
+                nc.tensor.matmul_mx(
+                    out=bank[:],
+                    lhsT=w_code[:, e, 2 * P * k : 2 * P * (k + 1)].bitcast(E2M1X4),
+                    lhsT_scale=w_scale[:, e, P * k : P * (k + 1)],
+                    rhs=code[:].bitcast(E5M2X4),
+                    rhs_scale=scale[:],
+                    start=first,
+                    stop=not first,
+                )
+            dx[e, k] = tile
+            nc.scalar.copy(tile, bank[:])
+
+        def spent_block(e, b):
+            return relu_a1[e][:, P * b : P * (b + 1), :].rearrange("p c t -> p (c t)")
+
+        def dx_tile():
+            return ring.tile([P, C], F32, name="dx_ring")[:]
 
         windows = {}
 
         def scatter(e, k):
             if k not in windows:
                 windows[k] = token_wide.tile([P, T], F32, name="token_wide_tile")
-            nc.vector.tensor_copy(windows[k][:].indirect(entries(e)), dx[e, k][:])
+            nc.vector.tensor_copy(windows[k][:].indirect(entries(e)), dx[e, k])
 
         gather(0)
         gather(1)
+        apply_relu(0)
+        relu_slope(0)
         quantise_gradients(0)
         gather(2)
         gather(3)
         quantise_gradients(1)
         for e in range(E):
-            apply_relu(e)
+            last = e == E - 1
+            if e > 0:
+                apply_relu(e)
             hidden_gradients(e)
             if e == 0:
                 load_a1(3)
-                load_a3(3)
-            else:
-                output_gradients(e - 1)
-            if 0 < e < E - 1:
+                quantise_hidden_gradients(e)
+                continue
+            if not last:
                 quantise_gradients(e + 1)
+            if e == 1:
+                load_a3(3)
             relu_slope(e)
-            if e > 0:
-                scatter(e - 1, 0)
-            if 0 < e < E - 1:
+            output_gradients(e - 1, 0, spent_block(e, 1))
+            if not last:
+                output_gradients(e - 1, 1, in_turn.tile([P, C], F32, name="da1_code", align_bytes=64)[:])
+            scatter(e - 1, 0)
+            if not last:
                 scatter(e - 1, 1)
             quantise_hidden_gradients(e)
+        spent = zero_one[E - 1][:].rearrange("p c t -> p (c t)").bitcast(F32)
+        output_gradients(E - 2, 1, spent[:, 0:C])
         scatter(E - 2, 1)
-        output_gradients(E - 1)
+        for k in range(K_BLOCKS):
+            output_gradients(E - 1, k, dx_tile())
         for k in range(K_BLOCKS):
             scatter(E - 1, k)
             nc.sync.dma_start(out[k * P : (k + 1) * P, :], windows[k][:])

@@ -10,7 +10,7 @@ PACK = 4
 K_BLOCKS = K // P
 SLOT_BLOCKS = C // P
 LIST_ROWS = 16
-RUN = 4
+RUN = 2
 
 HALVES = (slice(0, C // 2), slice(C // 2, C))
 
@@ -81,8 +81,7 @@ def tile_moe_bdx_glu_relu_kernel(
         dy_planes = {}
         a1_saved, a3_saved = {}, {}
 
-        def load_gates(first, last):
-            columns = slice(first * C, (last + 1) * C)
+        def load_gates(columns):
             nc.sync.dma_start(gates[:, columns], gate[0:P, columns])
 
         def load_plane(j):
@@ -99,15 +98,14 @@ def tile_moe_bdx_glu_relu_kernel(
         def load_a3(e):
             load_saved(a3_saved, a3, e, "a3_saved")
 
-        load_gates(0, 0)
+        load_gates(slots(0))
         load_plane(0)
-        load_gates(1, 1)
+        load_gates(slice(C, 3 * C))
         load_plane(1)
         load_plane(2)
-        load_gates(2, 2)
         load_a1(0)
         load_plane(3)
-        load_gates(3, 3)
+        load_gates(slots(3))
         load_words(w2_code, w2_words)
         load_scales(w2_scale, w2_scales)
         load_a3(0)
@@ -141,8 +139,8 @@ def tile_moe_bdx_glu_relu_kernel(
 
         first_and_last = held.tile([P, PACK + 1, C], F32, name="first_and_last")
         gradients = {0: first_and_last[:, 1:, :], E - 1: first_and_last[:, :PACK, :]}
-        for e in range(1, E - 1):
-            gradients[e] = held.tile([P, PACK, C], F32, name=f"gradients_{e}")[:]
+        middle = held.tile([P, PACK, 2 * C], F32, name="middle")
+        gradients[1], gradients[2] = middle[:, :, :C], middle[:, :, C:]
         gradient_codes, zero_one, dx = {}, {}, {}
 
         da1_codes, da3_codes, relu_a1, a3_first = {}, {}, {}, {}
@@ -150,11 +148,11 @@ def tile_moe_bdx_glu_relu_kernel(
         da1_tile = held.tile([P, C, PACK], BF16, name="da1_tile", align_bytes=64)
         da3_tile = held.tile([P, C, PACK], BF16, name="da3_tile", align_bytes=64)
 
-        def gather(e):
+        def gather(place, first, last):
+            columns = slice(first * C, (last + 1) * C)
+            chosen = offsets[:, columns.start // LIST_ROWS : columns.stop // LIST_ROWS]
             for j in range(PACK):
-                nc.vector.tensor_tensor(
-                    gradients[e][:, j, :], dy_planes[j][:].indirect(entries(e)), gates[:, slots(e)], MULT
-                )
+                nc.vector.tensor_tensor(place[:, j, :], dy_planes[j][:].indirect(chosen), gates[:, columns], MULT)
 
         def apply_relu(e):
             relu_a1[e] = ring.tile([P, C, PACK], F32, name="relu_a1_tile")
@@ -247,13 +245,12 @@ def tile_moe_bdx_glu_relu_kernel(
                 windows[k] = token_wide.tile([P, T], F32, name="token_wide_tile")
             nc.vector.tensor_copy(windows[k][:].indirect(entries(e)), dx[e, k])
 
-        gather(0)
-        gather(1)
+        gather(gradients[0], 0, 0)
+        gather(middle[:], 1, 2)
         apply_relu(0)
         relu_slope(0)
         quantise_gradients(0)
-        gather(2)
-        gather(3)
+        gather(gradients[E - 1], E - 1, E - 1)
         quantise_gradients(1)
         for e in range(E):
             last = e == E - 1

@@ -51,7 +51,6 @@ def tile_moe_bdx_glu_relu_kernel(
             return slice(e * C, (e + 1) * C)
 
         offsets = held.tile([P, E * C // LIST_ROWS], U16, name="offsets")
-        nc.sync.dma_start(offsets[:], offs)
 
         def entries(e):
             return offsets[:, e * C // LIST_ROWS : (e + 1) * C // LIST_ROWS]
@@ -98,8 +97,9 @@ def tile_moe_bdx_glu_relu_kernel(
         def load_a3(e):
             load_saved(a3_saved, a3, e, "a3_saved")
 
-        load_gates(slots(0))
         load_plane(0)
+        nc.sync.dma_start(offsets[:], offs)
+        load_gates(slots(0))
         load_gates(slice(C, 3 * C))
         load_plane(1)
         load_plane(2)
@@ -280,4 +280,5 @@ def tile_moe_bdx_glu_relu_kernel(
             output_gradients(E - 1, k, dx_tile())
         for k in range(K_BLOCKS):
             scatter(E - 1, k)
-            nc.sync.dma_start(out[k * P : (k + 1) * P, :], windows[k][:])
+            for queue, half in ((nc.sync, slice(0, T // 2)), (nc.scalar, slice(T // 2, T))):
+                queue.dma_start(out[k * P : (k + 1) * P, half], windows[k][:, half])

@@ -269,9 +269,8 @@ def tile_moe_bdx_glu_relu_kernel(
             output_gradients(e - 1, 0, spent_block(e, 1))
             if not last:
                 output_gradients(e - 1, 1, in_turn.tile([P, C], F32, name="da1_code", align_bytes=64)[:])
-            scatter(e - 1, 0)
-            if not last:
                 scatter(e - 1, 1)
+            scatter(e - 1, 0)
             quantise_hidden_gradients(e)
         spent = zero_one[E - 1][:].rearrange("p c t -> p (c t)").bitcast(F32)
         output_gradients(E - 2, 1, spent[:, 0:C])

@@ -71,17 +71,25 @@ def tile_moe_bdx_glu_relu_kernel(
         w1_scale = held.tile([P, E, K], U8, name="w1_scale", align_bytes=64)
         w3_code = held.tile([P, E, 2 * K], U8, name="w3_code", align_bytes=64)
         w3_scale = held.tile([P, E, K], U8, name="w3_scale", align_bytes=64)
-        for tile in (w2_scale, w1_scale, w3_scale):
-            nc.gpsimd.memset(tile[:].bitcast(I32), 0)
         identity = held.tile([P, P], F32, name="identity")
         make_identity(nc, identity[:])
+        for tile in (w2_scale, w1_scale, w3_scale):
+            nc.gpsimd.memset(tile[:].bitcast(I32), 0)
 
+        gate_columns = held.tile([P, E, 2 * PACK], F32, name="gate_columns")
+        nc.sync.dma_start(gate_columns[:, :, 0:PACK], gate[0, :].rearrange("(e p c) -> p e c", e=E, c=PACK))
         gates = held.tile([P, E * C], F32, name="gates")
         dy_planes = {}
         a1_saved, a3_saved = {}, {}
 
-        def load_gates(columns):
-            nc.sync.dma_start(gates[:, columns], gate[0:P, columns])
+        def spread_gates(e):
+            bank = (dh_banks if e else first_bank).tile([P, PACK, P], F32, name="dh")
+            for c in range(PACK):
+                nc.tensor.transpose(bank[:, c, :], gate_columns[:, e, c : c + 1].to_broadcast([P, P]), identity[:])
+            nc.scalar.copy(gates[:, slots(e)].rearrange("p (n c) -> p n c", c=PACK), bank[:].rearrange("p c n -> p n c"))
+
+        for e in (1, 2, 0, 3):
+            spread_gates(e)
 
         def load_plane(j):
             dy_planes[j] = token_wide.tile([P, T], F32, name="token_wide_tile")
@@ -99,13 +107,10 @@ def tile_moe_bdx_glu_relu_kernel(
 
         load_plane(0)
         nc.sync.dma_start(offsets[:], offs)
-        load_gates(slots(0))
-        load_gates(slice(C, 3 * C))
         load_plane(1)
         load_plane(2)
         load_a1(0)
         load_plane(3)
-        load_gates(slots(3))
         load_words(w2_code, w2_words)
         load_scales(w2_scale, w2_scales)
         load_a3(0)
@@ -138,7 +143,7 @@ def tile_moe_bdx_glu_relu_kernel(
             return mx_bank[b if e % 2 == 0 else SLOT_BLOCKS - 1 - b]
 
         first_and_last = held.tile([P, PACK + 1, C], F32, name="first_and_last")
-        gradients = {0: first_and_last[:, 1:, :], E - 1: first_and_last[:, :PACK, :]}
+        gradients = {0: first_and_last[:, :PACK, :], E - 1: first_and_last[:, 1:, :]}
         middle = held.tile([P, PACK, 2 * C], F32, name="middle")
         gradients[1], gradients[2] = middle[:, :, :C], middle[:, :, C:]
         gradient_codes, zero_one, dx = {}, {}, {}
@@ -148,10 +153,10 @@ def tile_moe_bdx_glu_relu_kernel(
         da1_tile = held.tile([P, C, PACK], BF16, name="da1_tile", align_bytes=64)
         da3_tile = held.tile([P, C, PACK], BF16, name="da3_tile", align_bytes=64)
 
-        def gather(place, first, last):
+        def gather(place, first, last, planes=range(PACK)):
             columns = slice(first * C, (last + 1) * C)
             chosen = offsets[:, columns.start // LIST_ROWS : columns.stop // LIST_ROWS]
-            for j in range(PACK):
+            for j in planes:
                 nc.vector.tensor_tensor(place[:, j, :], dy_planes[j][:].indirect(chosen), gates[:, columns], MULT)
 
         def apply_relu(e):
@@ -245,8 +250,9 @@ def tile_moe_bdx_glu_relu_kernel(
                 windows[k] = token_wide.tile([P, T], F32, name="token_wide_tile")
             nc.vector.tensor_copy(windows[k][:].indirect(entries(e)), dx[e, k])
 
-        gather(gradients[0], 0, 0)
-        gather(middle[:], 1, 2)
+        for j in range(PACK):
+            gather(gradients[0], 0, 0, [j])
+            gather(middle[:], 1, 2, [j])
         apply_relu(0)
         relu_slope(0)
         quantise_gradients(0)

@@ -14,6 +14,8 @@ RUN = 2
 
 HALVES = (slice(0, C // 2), slice(C // 2, C))
 
+BESIDE_SCATTERS = (1, 2)
+
 FLOPS = 2 * E * C * (N * H + 2 * H * K)
 WEIGHTS = E * (N * H + 2 * H * K)
 BYTES = 4 * (N * T + 2 * H * E * C + E * C + K * T) + WEIGHTS // 2 + WEIGHTS // 32 + 2 * P * (E * C // LIST_ROWS)
@@ -86,7 +88,8 @@ def tile_moe_bdx_glu_relu_kernel(
             bank = (dh_banks if e else first_bank).tile([P, PACK, P], F32, name="dh")
             for c in range(PACK):
                 nc.tensor.transpose(bank[:, c, :], gate_columns[:, e, c : c + 1].to_broadcast([P, P]), identity[:])
-            nc.scalar.copy(gates[:, slots(e)].rearrange("p (n c) -> p n c", c=PACK), bank[:].rearrange("p c n -> p n c"))
+            copy = nc.vector.tensor_copy if e == 1 else nc.scalar.copy
+            copy(gates[:, slots(e)].rearrange("p (n c) -> p n c", c=PACK), bank[:].rearrange("p c n -> p n c"))
 
         for e in (1, 2, 0, 3):
             spread_gates(e)
@@ -167,7 +170,10 @@ def tile_moe_bdx_glu_relu_kernel(
             nc.scalar.activation(to_columns(a3_first[e][:]), from_rows(a3_saved[e][:, :, 0:P]), COPY)
 
         def relu_slope(e):
-            zero_one[e] = ring.tile([P, C, PACK], BF16, name="zero_one_tile")
+            if e in BESIDE_SCATTERS:
+                zero_one[e] = in_turn.tile([P, C, PACK], BF16, name=f"da3_{e}_code", align_bytes=64)
+            else:
+                zero_one[e] = ring.tile([P, C, PACK], BF16, name="zero_one_tile")
             for half in HALVES:
                 nc.scalar.activation(zero_one[e][:, half, :], relu_a1[e][:, half, :], SIGN)
 
@@ -207,16 +213,20 @@ def tile_moe_bdx_glu_relu_kernel(
                     nc.gpsimd.tensor_tensor(da1_tile[:, block, :], dh_first[:], a3_first[e][:], MULT)
                     nc.gpsimd.tensor_tensor(da3_tile[:, block, :], dh_first[:], relu_a1[e][:, block, :], MULT)
                     continue
-                nc.vector.tensor_tensor(
-                    da3_tile[:, block, :], dh[:].rearrange("p t c -> p c t"), relu_a1[e][:, block, :], MULT
-                )
-                nc.vector.tensor_tensor(
-                    to_columns(da1_tile[:, block, :]), from_rows(dh[:]), from_rows(a3_saved[e][:, :, block]), MULT
-                )
+                products = [
+                    (da3_tile[:, block, :], dh[:].rearrange("p t c -> p c t"), relu_a1[e][:, block, :]),
+                    (to_columns(da1_tile[:, block, :]), from_rows(dh[:]), from_rows(a3_saved[e][:, :, block])),
+                ]
+                for product, factor, other in reversed(products) if b == SLOT_BLOCKS - 1 and e not in BESIDE_SCATTERS else products:
+                    nc.vector.tensor_tensor(product, factor, other, MULT)
 
         def quantise_hidden_gradients(e):
-            nc.vector.tensor_tensor(da1_tile[:], da1_tile[:], zero_one[e][:], MULT)
-            da3_codes[e] = quantise(da3_tile[:], "da3", ring)
+            engine = nc.gpsimd if e in BESIDE_SCATTERS else nc.vector
+            engine.tensor_tensor(da1_tile[:], da1_tile[:], zero_one[e][:], MULT)
+            if e in BESIDE_SCATTERS:
+                da3_codes[e] = quantise(da3_tile[:], f"da3_{e}", in_turn)
+            else:
+                da3_codes[e] = quantise(da3_tile[:], "da3", ring)
             da1_codes[e] = quantise(da1_tile[:], "da1", in_turn if e < E - 1 else ring)
 
         def output_gradients(e, k, tile):

@@ -16,6 +16,8 @@ HALVES = (slice(0, C // 2), slice(C // 2, C))
 
 BESIDE_SCATTERS = (1, 2)
 
+FIRST_BLOCKS = {0: 1, 1: 1, 2: 1, 3: 2}
+
 FLOPS = 2 * E * C * (N * H + 2 * H * K)
 WEIGHTS = E * (N * H + 2 * H * K)
 BYTES = 4 * (N * T + 2 * H * E * C + E * C + K * T) + WEIGHTS // 2 + WEIGHTS // 32 + 2 * P * (E * C // LIST_ROWS)
@@ -149,7 +151,7 @@ def tile_moe_bdx_glu_relu_kernel(
         gradients = {0: first_and_last[:, :PACK, :], E - 1: first_and_last[:, 1:, :]}
         middle = held.tile([P, PACK, 2 * C], F32, name="middle")
         gradients[1], gradients[2] = middle[:, :, :C], middle[:, :, C:]
-        gradient_codes, zero_one, dx = {}, {}, {}
+        gradient_codes, zero_one, dx, last_runs = {}, {}, {}, {}
 
         da1_codes, da3_codes, relu_a1, a3_first = {}, {}, {}, {}
 
@@ -164,10 +166,11 @@ def tile_moe_bdx_glu_relu_kernel(
 
         def apply_relu(e):
             relu_a1[e] = ring.tile([P, C, PACK], F32, name="relu_a1_tile")
-            a3_first[e] = ring.tile([P, P, PACK], F32, name="a3_first_tile")
+            first = slice(0, P * FIRST_BLOCKS[e])
+            a3_first[e] = ring.tile([P, first.stop, PACK], F32, name="a3_first_tile")
             for half in HALVES:
                 nc.scalar.activation(to_columns(relu_a1[e][:, half, :]), from_rows(a1_saved[e][:, :, half]), RELU)
-            nc.scalar.activation(to_columns(a3_first[e][:]), from_rows(a3_saved[e][:, :, 0:P]), COPY)
+            nc.scalar.activation(to_columns(a3_first[e][:]), from_rows(a3_saved[e][:, :, first]), COPY)
 
         def relu_slope(e):
             if e in BESIDE_SCATTERS:
@@ -202,15 +205,15 @@ def tile_moe_bdx_glu_relu_kernel(
                     start=True,
                     stop=True,
                 )
-                runs = by_slot_runs.tile([P, PACK, P], F32, name="runs")
+                runs = last_runs[e] = by_slot_runs.tile([P, PACK, P], F32, name="runs")
                 nc.scalar.copy(runs[:], by_slot[:].rearrange("p (m t) -> p t m", t=PACK))
                 dh = (dh_banks if b else first_bank).tile([P, PACK, P], F32, name="dh")
                 for t in range(PACK):
                     nc.tensor.transpose(dh[:, t, :], runs[:, t, :], identity[:])
-                if b == 0:
+                if b < FIRST_BLOCKS[e]:
                     dh_first = ring.tile([P, P, PACK], F32, name="dh_first")
                     nc.scalar.copy(dh_first[:], dh[:].rearrange("p t c -> p c t"))
-                    nc.gpsimd.tensor_tensor(da1_tile[:, block, :], dh_first[:], a3_first[e][:], MULT)
+                    nc.gpsimd.tensor_tensor(da1_tile[:, block, :], dh_first[:], a3_first[e][:, block, :], MULT)
                     nc.gpsimd.tensor_tensor(da3_tile[:, block, :], dh_first[:], relu_a1[e][:, block, :], MULT)
                     continue
                 products = [
@@ -222,7 +225,8 @@ def tile_moe_bdx_glu_relu_kernel(
 
         def quantise_hidden_gradients(e):
             engine = nc.gpsimd if e in BESIDE_SCATTERS else nc.vector
-            engine.tensor_tensor(da1_tile[:], da1_tile[:], zero_one[e][:], MULT)
+            for part in HALVES if e in BESIDE_SCATTERS else [slice(0, C)]:
+                engine.tensor_tensor(da1_tile[:, part, :], da1_tile[:, part, :], zero_one[e][:, part, :], MULT)
             if e in BESIDE_SCATTERS:
                 da3_codes[e] = quantise(da3_tile[:], f"da3_{e}", in_turn)
             else:
@@ -246,9 +250,6 @@ def tile_moe_bdx_glu_relu_kernel(
                 )
             dx[e, k] = tile
             nc.scalar.copy(tile, bank[:])
-
-        def spent_block(e, b):
-            return relu_a1[e][:, P * b : P * (b + 1), :].rearrange("p c t -> p (c t)")
 
         def dx_tile():
             return ring.tile([P, C], F32, name="dx_ring")[:]
@@ -281,12 +282,12 @@ def tile_moe_bdx_glu_relu_kernel(
                 quantise_gradients(e + 1)
             if e == 1:
                 load_a3(3)
-            relu_slope(e)
-            output_gradients(e - 1, 0, spent_block(e, 1))
+            output_gradients(e - 1, 0, last_runs[e][:].rearrange("p t m -> p (t m)"))
             if not last:
                 output_gradients(e - 1, 1, in_turn.tile([P, C], F32, name="da1_code", align_bytes=64)[:])
                 scatter(e - 1, 1)
             scatter(e - 1, 0)
+            relu_slope(e)
             quantise_hidden_gradients(e)
         spent = zero_one[E - 1][:].rearrange("p c t -> p (c t)").bitcast(F32)
         output_gradients(E - 2, 1, spent[:, 0:C])

@@ -8,15 +8,13 @@ K, T, E, C, H, N = 256, 2048, 4, 512, 512, 512
 P = 128
 PACK = 4
 K_BLOCKS = K // P
-SLOT_BLOCKS = C // P
 LIST_ROWS = 16
-RUN = 2
-
-HALVES = (slice(0, C // 2), slice(C // 2, C))
-
-BESIDE_SCATTERS = (1, 2)
-
-FIRST_BLOCKS = {0: 1, 1: 1, 2: 1, 3: 2}
+CHUNK = 256
+CHUNKS = E * C // CHUNK
+BLOCKS = CHUNK // P
+RUN = 4
+GATED = 3
+EARLY = 6
 
 FLOPS = 2 * E * C * (N * H + 2 * H * K)
 WEIGHTS = E * (N * H + 2 * H * K)
@@ -31,9 +29,9 @@ U8 = mybir.dt.uint8
 E5M2X4 = mybir.dt.float8_e5m2_x4
 E2M1X4 = mybir.dt.float4_e2m1fn_x4
 MULT = mybir.AluOpType.mult
+MAX = mybir.AluOpType.max
+IS_GT = mybir.AluOpType.is_gt
 COPY = mybir.ActivationFunctionType.Copy
-RELU = mybir.ActivationFunctionType.Relu
-SIGN = mybir.ActivationFunctionType.Sign
 
 
 def tile_moe_bdx_glu_relu_kernel(
@@ -42,25 +40,24 @@ def tile_moe_bdx_glu_relu_kernel(
     nc = tc.nc
     with ExitStack() as ctx:
         held = ctx.enter_context(tc.tile_pool(name="held", bufs=1))
-        token_wide = ctx.enter_context(tc.tile_pool(name="token_wide", bufs=PACK))
+        ring = ctx.enter_context(tc.tile_pool(name="ring", bufs=3))
+        before_w2 = ctx.enter_context(tc.tile_pool(name="before_w2", bufs=1))
+        after_gated = ctx.enter_context(tc.tile_pool(name="after_gated", bufs=1))
+        pairs = ctx.enter_context(tc.tile_pool(name="pairs", bufs=2))
         in_turn = ctx.enter_context(tc.tile_pool(name="in_turn", bufs=1))
-        ring = ctx.enter_context(tc.tile_pool(name="ring", bufs=2))
-        saved = ctx.enter_context(tc.tile_pool(name="saved", bufs=3))
-        by_slot_runs = ctx.enter_context(tc.tile_pool(name="by_slot_runs", bufs=8))
-        mx_banks = ctx.enter_context(tc.psum_pool(name="mx_banks", bufs=1))
-        first_bank = ctx.enter_context(tc.psum_pool(name="first_bank", bufs=1))
-        dh_banks = ctx.enter_context(tc.psum_pool(name="dh_banks", bufs=SLOT_BLOCKS - 1))
-
-        def slots(e):
-            return slice(e * C, (e + 1) * C)
+        dh_banks = ctx.enter_context(tc.psum_pool(name="dh_banks", bufs=2 * BLOCKS))
+        dx_banks = ctx.enter_context(tc.psum_pool(name="dx_banks", bufs=2))
+        gate_banks = ctx.enter_context(tc.psum_pool(name="gate_banks", bufs=2))
 
         offsets = held.tile([P, E * C // LIST_ROWS], U16, name="offsets")
 
-        def entries(e):
-            return offsets[:, e * C // LIST_ROWS : (e + 1) * C // LIST_ROWS]
+        def entries(first, count):
+            return offsets[:, first // LIST_ROWS : (first + count) // LIST_ROWS]
 
-        def load_words(tile, dram):
-            nc.sync.dma_start(tile[:].bitcast(I32), dram.rearrange("e s p b -> p (e s) b").bitcast(I32))
+        def load_words(name, dram, first, last):
+            tile = held.tile([P, last - first, dram.shape[3]], U8, name=name, align_bytes=64)
+            nc.sync.dma_start(tile[:].bitcast(I32), dram[first:last].rearrange("e s p b -> p (e s) b").bitcast(I32))
+            return tile
 
         def load_scales(tile, dram):
             for q in range(4):
@@ -69,232 +66,244 @@ def tile_moe_bdx_glu_relu_kernel(
                     dram[:, 0, 4 * q : 4 * q + 4, :].rearrange("e f i -> f e i").bitcast(I32),
                 )
 
-        w2_code = held.tile([P, E, 2 * H], U8, name="w2_code", align_bytes=64)
-        w2_scale = held.tile([P, E, H], U8, name="w2_scale", align_bytes=64)
-        w1_code = held.tile([P, E, 2 * K], U8, name="w1_code", align_bytes=64)
+        w2_scale_raw = held.tile([P, E, H], U8, name="w2_scale_raw", align_bytes=64)
         w1_scale = held.tile([P, E, K], U8, name="w1_scale", align_bytes=64)
-        w3_code = held.tile([P, E, 2 * K], U8, name="w3_code", align_bytes=64)
         w3_scale = held.tile([P, E, K], U8, name="w3_scale", align_bytes=64)
+        nc.vector.memset(w2_scale_raw[:].bitcast(I32), 0)
         identity = held.tile([P, P], F32, name="identity")
         make_identity(nc, identity[:])
-        for tile in (w2_scale, w1_scale, w3_scale):
+        for tile in (w1_scale, w3_scale):
             nc.gpsimd.memset(tile[:].bitcast(I32), 0)
 
-        gate_columns = held.tile([P, E, 2 * PACK], F32, name="gate_columns")
-        nc.sync.dma_start(gate_columns[:, :, 0:PACK], gate[0, :].rearrange("(e p c) -> p e c", e=E, c=PACK))
-        gates = held.tile([P, E * C], F32, name="gates")
-        dy_planes = {}
-        a1_saved, a3_saved = {}, {}
+        gate_columns = {}
 
-        def spread_gates(e):
-            bank = (dh_banks if e else first_bank).tile([P, PACK, P], F32, name="dh")
-            for c in range(PACK):
-                nc.tensor.transpose(bank[:, c, :], gate_columns[:, e, c : c + 1].to_broadcast([P, P]), identity[:])
-            copy = nc.vector.tensor_copy if e == 1 else nc.scalar.copy
-            copy(gates[:, slots(e)].rearrange("p (n c) -> p n c", c=PACK), bank[:].rearrange("p c n -> p n c"))
+        def load_gates(first, tile):
+            row = gate[0, first * C : (first + 2) * C]
+            nc.sync.dma_start(tile[:, :, 0:PACK], row.rearrange("(e p c) -> p e c", e=2, c=PACK))
+            gate_columns[first], gate_columns[first + 1] = tile[:, 0], tile[:, 1]
 
-        for e in (1, 2, 0, 3):
-            spread_gates(e)
+        load_gates(0, before_w2.tile([P, 2, H + 8], F32, name="gate_columns", align_bytes=64, offset=0))
+        load_scales(w2_scale_raw, w2_scales)
+
+        planes = {}
 
         def load_plane(j):
-            dy_planes[j] = token_wide.tile([P, T], F32, name="token_wide_tile")
-            nc.sync.dma_start(dy_planes[j][:], dyT.rearrange("(p j) s -> p j s", j=PACK)[:, j, :])
+            planes[j] = held.tile([P, T], F32, name=f"plane_{j}")
+            nc.sync.dma_start(planes[j][:], dyT.rearrange("(p j) s -> p j s", j=PACK)[:, j, :])
 
-        def load_saved(tiles, dram, e, name):
-            tiles[e] = saved.tile([P, PACK, C], F32, name=name, align_bytes=64)
-            nc.sync.dma_start(tiles[e][:], dram.rearrange("(p t) s -> p t s", t=PACK)[:, :, slots(e)])
+        saved = {}
 
-        def load_a1(e):
-            load_saved(a1_saved, a1, e, "a1_saved")
-
-        def load_a3(e):
-            load_saved(a3_saved, a3, e, "a3_saved")
+        def load_saved(name, dram, first, count):
+            tile = held.tile([P, PACK, count], F32, name=f"{name}_{first}", align_bytes=64)
+            nc.sync.dma_start(tile[:], dram.rearrange("(p t) s -> p t s", t=PACK)[:, :, first : first + count])
+            for c in range(count // CHUNK):
+                saved[name, first // CHUNK + c] = tile[:, :, c * CHUNK : (c + 1) * CHUNK]
 
         load_plane(0)
         nc.sync.dma_start(offsets[:], offs)
         load_plane(1)
+        w2_raw = {0: load_words("w2_raw_0", w2_words, 0, 2)}
         load_plane(2)
-        load_a1(0)
         load_plane(3)
-        load_words(w2_code, w2_words)
-        load_scales(w2_scale, w2_scales)
-        load_a3(0)
-        load_a1(1)
-        load_a3(1)
-        load_words(w1_code, w1_words)
-        load_words(w3_code, w3_words)
+        load_gates(2, held.tile([P, 2, 2 * PACK], F32, name="gate_columns_late"))
+        for first in (0, CHUNK):
+            load_saved("a1", a1, first, CHUNK)
+            load_saved("a3", a3, first, CHUNK)
+        w2_raw[2] = load_words("w2_raw_2", w2_words, 2, E)
+        w1_code = load_words("w1_code", w1_words, 0, E)
+        w3_code = load_words("w3_code", w3_words, 0, E)
         load_scales(w1_scale, w1_scales)
         load_scales(w3_scale, w3_scales)
-        load_a1(2)
-        load_a3(2)
+        for e in range(1, E):
+            load_saved("a1", a1, e * C, C)
+            load_saved("a3", a3, e * C, C)
+
+        def spread_gates(e, pool, name):
+            bank = pool.tile([P, PACK, P], F32, name=name)
+            for c in range(PACK):
+                nc.tensor.transpose(bank[:, c, :], gate_columns[e][:, c : c + 1].to_broadcast([P, P]), identity[:])
+            return bank[:].rearrange("p c n -> p n c")
+
+        gates = held.tile([P, 2 * C], F32, name="gates")
+        for e in range(2):
+            place = gates[:, e * C : (e + 1) * C].rearrange("p (n c) -> p n c", c=PACK)
+            if e == 0:
+                nc.vector.tensor_copy(place, spread_gates(e, dx_banks, "dx"))
+            else:
+                nc.scalar.activation(place, spread_gates(e, dx_banks, "dx"), COPY)
+        gates_in_psum = {e: spread_gates(e, gate_banks, "gate_bank") for e in range(2, E)}
+
+        w2_scale = before_w2.tile([P, E, H], U8, name="w2_scale", align_bytes=64, offset=4 * H)
+        nc.vector.tensor_copy(
+            w2_scale[:].rearrange("p e (t m) -> p e t m", t=PACK), w2_scale_raw[:].rearrange("p e (m t) -> p e t m", t=PACK)
+        )
+        w2_code = {}
+
+        def permute_w2(e):
+            if e < 2:
+                pool, offset = before_w2, e * 2 * H
+            else:
+                pool, offset = after_gated, 4 * PACK * (CHUNKS - EARLY) * CHUNK + (e - 2) * 2 * H
+            w2_code[e] = pool.tile([P, 2 * H], U8, name=f"w2_code_{e}", align_bytes=64, offset=offset)
+            nc.scalar.copy(
+                w2_code[e][:].bitcast(U16).rearrange("p (t m) -> p t m", t=PACK),
+                w2_raw[e - e % 2][:, e % 2, :].bitcast(U16).rearrange("p (m t) -> p t m", t=PACK),
+            )
 
         def from_rows(ap):
-            return ap.rearrange("p t (c i) -> p c t i", i=RUN)
+            return ap.rearrange("p t (n c) -> p n t c", c=RUN)
 
         def to_columns(ap):
-            return ap.rearrange("p (c i) t -> p c t i", i=RUN)
+            return ap.rearrange("p (n c) t -> p n t c", c=RUN)
 
-        def quantise(values, name, pool):
-            code = pool.tile([P, C], U32, name=name + "_code", align_bytes=64)
-            scale = ring.tile([P, C], U8, name=name + "_scale", align_bytes=64)
-            nc.vector.quantize_mx(
-                out=code[:].bitcast(E5M2X4), scales=scale[:], in_=values.rearrange("p c t -> p (c t)")
+        gated = after_gated.tile([P, PACK, GATED * CHUNK], F32, name="gated", align_bytes=64, offset=0)
+        ungated = {
+            GATED: before_w2.tile(
+                [P, PACK, (EARLY - GATED) * CHUNK], F32, name="ungated_early", align_bytes=64, offset=8 * H
             )
+        }
+
+        def gather_gated(j, first, last):
+            columns = slice(first * CHUNK, last * CHUNK)
+            chosen = entries(columns.start, columns.stop - columns.start)
+            nc.vector.tensor_tensor(gated[:, j, columns], planes[j][:].indirect(chosen), gates[:, columns], MULT)
+
+        def gather_ungated(j, first, last):
+            base = GATED if first < EARLY else EARLY
+            place = ungated[base][:, j, (first - base) * CHUNK : (last - base) * CHUNK]
+            nc.scalar.activation(place, planes[j][:].indirect(entries(first * CHUNK, (last - first) * CHUNK)), COPY)
+
+        rounded, dh, da, masked = {}, {}, {}, {}
+
+        def round_gated(c):
+            rounded[c] = held.tile([P, CHUNK, PACK], BF16, name=f"rounded_{c}", align_bytes=64)
+            nc.scalar.activation(to_columns(rounded[c][:]), from_rows(gated[:, :, c * CHUNK : (c + 1) * CHUNK]), COPY)
+
+        def gate_and_round(block):
+            c, b = divmod(block, BLOCKS)
+            if b == 0:
+                rounded[c] = ring.tile([P, CHUNK, PACK], BF16, name="rounded_late", align_bytes=64)
+            e, first = divmod(block * P, C)
+            base = GATED if c < EARLY else EARLY
+            rows = ungated[base][:, :, block * P - base * CHUNK : (block + 1) * P - base * CHUNK]
+            if e in gates_in_psum:
+                factor = gates_in_psum[e][:, first // RUN : (first + P) // RUN, :]
+            else:
+                factor = gates[:, block * P : (block + 1) * P].rearrange("p (n c) -> p n c", c=RUN)
+            factor = factor.unsqueeze(2).broadcast_to([P, P // RUN, PACK, RUN])
+            nc.vector.tensor_tensor(to_columns(rounded[c][:, b * P : (b + 1) * P, :]), from_rows(rows), factor, MULT)
+
+        def quantise(values, columns, name):
+            code = ring.tile([P, columns], U32, name=name + "_code", align_bytes=64)
+            scale = ring.tile([P, columns], U8, name=name + "_scale", align_bytes=64)
+            nc.vector.quantize_mx(out=code[:].bitcast(E5M2X4), scales=scale[:], in_=values)
             return code, scale
 
-        mx_bank = [mx_banks.tile([P, C], F32, name=f"mx_bank_{n}") for n in range(SLOT_BLOCKS)]
-
-        def mx_bank_of(e, b):
-            return mx_bank[b if e % 2 == 0 else SLOT_BLOCKS - 1 - b]
-
-        first_and_last = held.tile([P, PACK + 1, C], F32, name="first_and_last")
-        gradients = {0: first_and_last[:, :PACK, :], E - 1: first_and_last[:, 1:, :]}
-        middle = held.tile([P, PACK, 2 * C], F32, name="middle")
-        gradients[1], gradients[2] = middle[:, :, :C], middle[:, :, C:]
-        gradient_codes, zero_one, dx, last_runs = {}, {}, {}, {}
-
-        da1_codes, da3_codes, relu_a1, a3_first = {}, {}, {}, {}
-
-        da1_tile = held.tile([P, C, PACK], BF16, name="da1_tile", align_bytes=64)
-        da3_tile = held.tile([P, C, PACK], BF16, name="da3_tile", align_bytes=64)
-
-        def gather(place, first, last, planes=range(PACK)):
-            columns = slice(first * C, (last + 1) * C)
-            chosen = offsets[:, columns.start // LIST_ROWS : columns.stop // LIST_ROWS]
-            for j in planes:
-                nc.vector.tensor_tensor(place[:, j, :], dy_planes[j][:].indirect(chosen), gates[:, columns], MULT)
-
-        def apply_relu(e):
-            relu_a1[e] = ring.tile([P, C, PACK], F32, name="relu_a1_tile")
-            first = slice(0, P * FIRST_BLOCKS[e])
-            a3_first[e] = ring.tile([P, first.stop, PACK], F32, name="a3_first_tile")
-            for half in HALVES:
-                nc.scalar.activation(to_columns(relu_a1[e][:, half, :]), from_rows(a1_saved[e][:, :, half]), RELU)
-            nc.scalar.activation(to_columns(a3_first[e][:]), from_rows(a3_saved[e][:, :, first]), COPY)
-
-        def relu_slope(e):
-            if e in BESIDE_SCATTERS:
-                zero_one[e] = in_turn.tile([P, C, PACK], BF16, name=f"da3_{e}_code", align_bytes=64)
-            else:
-                zero_one[e] = ring.tile([P, C, PACK], BF16, name="zero_one_tile")
-            for half in HALVES:
-                nc.scalar.activation(zero_one[e][:, half, :], relu_a1[e][:, half, :], SIGN)
-
-        def quantise_gradients(e):
-            if e == 1:
-                rounded = da1_tile[:]
-            elif e == 0:
-                rounded = da3_tile[:]
-            else:
-                rows = a3_saved[e - 2][:, 0:2, :].rearrange("p t c -> p (t c)")
-                rounded = rows.bitcast(BF16).rearrange("p (c t) -> p c t", t=PACK)
-            nc.scalar.activation(to_columns(rounded), from_rows(gradients[e]), COPY)
-            gradient_codes[e] = quantise(rounded, "g", ring)
-
-        def hidden_gradients(e):
-            code, scale = gradient_codes[e]
-            for b in range(SLOT_BLOCKS):
-                block = slice(P * b, P * (b + 1))
-                by_slot = mx_bank_of(e, b)
-                nc.tensor.matmul_mx(
-                    out=by_slot[:],
-                    lhsT=code[:, block].bitcast(E5M2X4),
-                    lhsT_scale=scale[:, block],
-                    rhs=w2_code[:, e, :].bitcast(E2M1X4),
-                    rhs_scale=w2_scale[:, e, :],
-                    start=True,
-                    stop=True,
-                )
-                runs = last_runs[e] = by_slot_runs.tile([P, PACK, P], F32, name="runs")
-                nc.scalar.copy(runs[:], by_slot[:].rearrange("p (m t) -> p t m", t=PACK))
-                dh = (dh_banks if b else first_bank).tile([P, PACK, P], F32, name="dh")
+        def hidden_gradient(c):
+            e = c * CHUNK // C
+            code, scale = quantise(rounded[c][:].rearrange("p c t -> p (c t)"), CHUNK, "g")
+            for b in range(BLOCKS):
+                block = slice(b * P, (b + 1) * P)
+                bank = dh[c, b] = dh_banks.tile([P, PACK, P], F32, name="dh")
                 for t in range(PACK):
-                    nc.tensor.transpose(dh[:, t, :], runs[:, t, :], identity[:])
-                if b < FIRST_BLOCKS[e]:
-                    dh_first = ring.tile([P, P, PACK], F32, name="dh_first")
-                    nc.scalar.copy(dh_first[:], dh[:].rearrange("p t c -> p c t"))
-                    nc.gpsimd.tensor_tensor(da1_tile[:, block, :], dh_first[:], a3_first[e][:, block, :], MULT)
-                    nc.gpsimd.tensor_tensor(da3_tile[:, block, :], dh_first[:], relu_a1[e][:, block, :], MULT)
-                    continue
-                products = [
-                    (da3_tile[:, block, :], dh[:].rearrange("p t c -> p c t"), relu_a1[e][:, block, :]),
-                    (to_columns(da1_tile[:, block, :]), from_rows(dh[:]), from_rows(a3_saved[e][:, :, block])),
-                ]
-                for product, factor, other in reversed(products) if b == SLOT_BLOCKS - 1 and e not in BESIDE_SCATTERS else products:
-                    nc.vector.tensor_tensor(product, factor, other, MULT)
+                    nc.tensor.matmul_mx(
+                        out=bank[:, t, :],
+                        lhsT=w2_code[e][:, 2 * P * t : 2 * P * (t + 1)].bitcast(E2M1X4),
+                        lhsT_scale=w2_scale[:, e, P * t : P * (t + 1)],
+                        rhs=code[:, block].bitcast(E5M2X4),
+                        rhs_scale=scale[:, block],
+                        start=True,
+                        stop=True,
+                    )
 
-        def quantise_hidden_gradients(e):
-            engine = nc.gpsimd if e in BESIDE_SCATTERS else nc.vector
-            for part in HALVES if e in BESIDE_SCATTERS else [slice(0, C)]:
-                engine.tensor_tensor(da1_tile[:, part, :], da1_tile[:, part, :], zero_one[e][:, part, :], MULT)
-            if e in BESIDE_SCATTERS:
-                da3_codes[e] = quantise(da3_tile[:], f"da3_{e}", in_turn)
-            else:
-                da3_codes[e] = quantise(da3_tile[:], "da3", ring)
-            da1_codes[e] = quantise(da1_tile[:], "da1", in_turn if e < E - 1 else ring)
-
-        def output_gradients(e, k, tile):
-            bank = mx_bank_of(min(e + 1, E - 1), SLOT_BLOCKS - K_BLOCKS + k)
-            for w_code, w_scale, (code, scale), first in (
-                (w3_code, w3_scale, da3_codes[e], True),
-                (w1_code, w1_scale, da1_codes[e], False),
-            ):
-                nc.tensor.matmul_mx(
-                    out=bank[:],
-                    lhsT=w_code[:, e, 2 * P * k : 2 * P * (k + 1)].bitcast(E2M1X4),
-                    lhsT_scale=w_scale[:, e, P * k : P * (k + 1)],
-                    rhs=code[:].bitcast(E5M2X4),
-                    rhs_scale=scale[:],
-                    start=first,
-                    stop=not first,
+        def mask(c):
+            masked[c] = pairs.tile([P, PACK, CHUNK], F32, name="masked", align_bytes=64)
+            for b in range(BLOCKS):
+                nc.vector.scalar_tensor_tensor(
+                    masked[c][:, :, b * P : (b + 1) * P], saved["a1", c][:, :, b * P : (b + 1) * P], 0.0, dh[c, b][:], IS_GT, MULT
                 )
-            dx[e, k] = tile
-            nc.scalar.copy(tile, bank[:])
 
-        def dx_tile():
-            return ring.tile([P, C], F32, name="dx_ring")[:]
+        def products(c):
+            da[c] = in_turn.tile([P, 2, CHUNK, PACK], BF16, name="da", align_bytes=64)
+            nc.gpsimd.tensor_tensor(
+                da[c][:, 0], masked[c][:].rearrange("p t c -> p c t"), saved["a3", c].rearrange("p t c -> p c t"), MULT
+            )
+            for b in range(BLOCKS):
+                block = slice(b * P, (b + 1) * P)
+                nc.vector.scalar_tensor_tensor(
+                    da[c][:, 1, block, :],
+                    saved["a1", c][:, :, block].rearrange("p t c -> p c t"),
+                    0.0,
+                    dh[c, b][:].rearrange("p t c -> p c t"),
+                    MAX,
+                    MULT,
+                )
 
-        windows = {}
+        windows = [held.tile([P, T], F32, name=f"window_{k}") for k in range(K_BLOCKS)]
 
-        def scatter(e, k):
-            if k not in windows:
-                windows[k] = token_wide.tile([P, T], F32, name="token_wide_tile")
-            nc.vector.tensor_copy(windows[k][:].indirect(entries(e)), dx[e, k])
+        def input_gradient(c):
+            e = c * CHUNK // C
+            last = c == CHUNKS - 1
+            code, scale = quantise(da[c][:].rearrange("p a c t -> p (a c t)"), 2 * CHUNK, "da")
+            dx = ring.tile([P, K_BLOCKS, CHUNK], F32, name="dx_out")
+            for k in range(K_BLOCKS):
+                if k == 0 or last:
+                    bank = dx_banks.tile([P, K_BLOCKS, CHUNK], F32, name="dx")
+                for a, (w_code, w_scale) in enumerate(((w1_code, w1_scale), (w3_code, w3_scale))):
+                    nc.tensor.matmul_mx(
+                        out=bank[:, k, :],
+                        lhsT=w_code[:, e, 2 * P * k : 2 * P * (k + 1)].bitcast(E2M1X4),
+                        lhsT_scale=w_scale[:, e, P * k : P * (k + 1)],
+                        rhs=code[:, a * CHUNK : (a + 1) * CHUNK].bitcast(E5M2X4),
+                        rhs_scale=scale[:, a * CHUNK : (a + 1) * CHUNK],
+                        start=a == 0,
+                        stop=a == 1,
+                    )
+                if last:
+                    copy = nc.vector.tensor_copy if k else nc.scalar.copy
+                    copy(dx[:, k, :], bank[:, k, :])
+            if not last:
+                nc.scalar.copy(dx[:], bank[:])
+            for k in range(K_BLOCKS):
+                place = windows[k][:].indirect(entries(c * CHUNK, CHUNK))
+                if last and k:
+                    nc.vector.tensor_copy(place, dx[:, k, :])
+                else:
+                    nc.scalar.activation(place, dx[:, k, :], COPY)
 
+        permute_w2(0)
+        permute_w2(1)
+        for j in range(PACK - 1):
+            gather_gated(j, 0, GATED)
+            gather_ungated(j, GATED, EARLY)
+        for c in range(GATED):
+            gather_gated(PACK - 1, c, c + 1)
+        gather_ungated(PACK - 1, GATED, GATED + 1)
+        round_gated(0)
+        round_gated(1)
+        gather_ungated(PACK - 1, GATED + 1, EARLY)
+        round_gated(2)
+        ungated[EARLY] = after_gated.tile(
+            [P, PACK, (CHUNKS - EARLY) * CHUNK], F32, name="ungated_late", align_bytes=64, offset=0
+        )
         for j in range(PACK):
-            gather(gradients[0], 0, 0, [j])
-            gather(middle[:], 1, 2, [j])
-        apply_relu(0)
-        relu_slope(0)
-        quantise_gradients(0)
-        gather(gradients[E - 1], E - 1, E - 1)
-        quantise_gradients(1)
-        for e in range(E):
-            last = e == E - 1
-            if e > 0:
-                apply_relu(e)
-            hidden_gradients(e)
-            if e == 0:
-                load_a1(3)
-                quantise_hidden_gradients(e)
-                continue
-            if not last:
-                quantise_gradients(e + 1)
-            if e == 1:
-                load_a3(3)
-            output_gradients(e - 1, 0, last_runs[e][:].rearrange("p t m -> p (t m)"))
-            if not last:
-                output_gradients(e - 1, 1, in_turn.tile([P, C], F32, name="da1_code", align_bytes=64)[:])
-                scatter(e - 1, 1)
-            scatter(e - 1, 0)
-            relu_slope(e)
-            quantise_hidden_gradients(e)
-        spent = zero_one[E - 1][:].rearrange("p c t -> p (c t)").bitcast(F32)
-        output_gradients(E - 2, 1, spent[:, 0:C])
-        scatter(E - 2, 1)
-        for k in range(K_BLOCKS):
-            output_gradients(E - 1, k, dx_tile())
-        for k in range(K_BLOCKS):
-            scatter(E - 1, k)
-            for queue, half in ((nc.sync, slice(0, T // 2)), (nc.scalar, slice(T // 2, T))):
-                queue.dma_start(out[k * P : (k + 1) * P, half], windows[k][:, half])
+            gather_ungated(j, EARLY, CHUNKS)
+        permute_w2(2)
+        permute_w2(3)
+        blocks = list(range(GATED * BLOCKS, CHUNKS * BLOCKS))
+        hidden_gradient(0)
+        gate_and_round(blocks.pop(0))
+        hidden_gradient(1)
+        gate_and_round(blocks.pop(0))
+        mask(0)
+        for c in range(CHUNKS):
+            products(c)
+            for block in blocks[: 2 if c < 2 else 1]:
+                gate_and_round(blocks.pop(0))
+            if c + 1 < CHUNKS:
+                mask(c + 1)
+            input_gradient(c)
+            if c + 2 < CHUNKS:
+                hidden_gradient(c + 2)
+        for k, queue in enumerate((nc.scalar, nc.sync)):
+            queue.dma_start(out[k * P : (k + 1) * P, :], windows[k][:])

@@ -99,10 +99,10 @@ def tile_moe_bdx_glu_relu_kernel(
             for c in range(count // CHUNK):
                 saved[name, first // CHUNK + c] = tile[:, :, c * CHUNK : (c + 1) * CHUNK]
 
+        w2_raw = {0: load_words("w2_raw_0", w2_words, 0, 2)}
         load_plane(0)
         nc.sync.dma_start(offsets[:], offs)
         load_plane(1)
-        w2_raw = {0: load_words("w2_raw_0", w2_words, 0, 2)}
         load_plane(2)
         load_plane(3)
         load_gates(2, held.tile([P, 2, 2 * PACK], F32, name="gate_columns_late"))
@@ -225,9 +225,7 @@ def tile_moe_bdx_glu_relu_kernel(
 
         def products(c):
             da[c] = in_turn.tile([P, 2, CHUNK, PACK], BF16, name="da", align_bytes=64)
-            nc.gpsimd.tensor_tensor(
-                da[c][:, 0], masked[c][:].rearrange("p t c -> p c t"), saved["a3", c].rearrange("p t c -> p c t"), MULT
-            )
+            nc.gpsimd.tensor_tensor(to_columns(da[c][:, 0]), from_rows(masked[c][:]), from_rows(saved["a3", c]), MULT)
             for b in range(BLOCKS):
                 block = slice(b * P, (b + 1) * P)
                 nc.vector.scalar_tensor_tensor(
@@ -266,7 +264,7 @@ def tile_moe_bdx_glu_relu_kernel(
                 nc.scalar.copy(dx[:], bank[:])
             for k in range(K_BLOCKS):
                 place = windows[k][:].indirect(entries(c * CHUNK, CHUNK))
-                if last and k:
+                if c >= CHUNKS - 2 and k:
                     nc.vector.tensor_copy(place, dx[:, k, :])
                 else:
                     nc.scalar.activation(place, dx[:, k, :], COPY)

@@ -13,8 +13,7 @@ CHUNK = 256
 CHUNKS = E * C // CHUNK
 BLOCKS = CHUNK // P
 RUN = 4
-GATED = 3
-EARLY = 6
+GATED = CHUNKS // 2
 
 FLOPS = 2 * E * C * (N * H + 2 * H * K)
 WEIGHTS = E * (N * H + 2 * H * K)
@@ -42,7 +41,7 @@ def tile_moe_bdx_glu_relu_kernel(
         held = ctx.enter_context(tc.tile_pool(name="held", bufs=1))
         ring = ctx.enter_context(tc.tile_pool(name="ring", bufs=3))
         before_w2 = ctx.enter_context(tc.tile_pool(name="before_w2", bufs=1))
-        after_gated = ctx.enter_context(tc.tile_pool(name="after_gated", bufs=1))
+        after_rounded = ctx.enter_context(tc.tile_pool(name="after_rounded", bufs=1))
         pairs = ctx.enter_context(tc.tile_pool(name="pairs", bufs=2))
         in_turn = ctx.enter_context(tc.tile_pool(name="in_turn", bufs=1))
         dh_banks = ctx.enter_context(tc.psum_pool(name="dh_banks", bufs=2 * BLOCKS))
@@ -106,14 +105,15 @@ def tile_moe_bdx_glu_relu_kernel(
         load_plane(2)
         load_plane(3)
         load_gates(2, held.tile([P, 2, 2 * PACK], F32, name="gate_columns_late"))
-        for first in (0, CHUNK):
-            load_saved("a1", a1, first, CHUNK)
-            load_saved("a3", a3, first, CHUNK)
+        load_saved("a1", a1, 0, CHUNK)
         w2_raw[2] = load_words("w2_raw_2", w2_words, 2, E)
+        load_saved("a3", a3, 0, CHUNK)
+        load_saved("a1", a1, CHUNK, CHUNK)
         w1_code = load_words("w1_code", w1_words, 0, E)
         w3_code = load_words("w3_code", w3_words, 0, E)
         load_scales(w1_scale, w1_scales)
         load_scales(w3_scale, w3_scales)
+        load_saved("a3", a3, CHUNK, CHUNK)
         for e in range(1, E):
             load_saved("a1", a1, e * C, C)
             load_saved("a3", a3, e * C, C)
@@ -143,7 +143,7 @@ def tile_moe_bdx_glu_relu_kernel(
             if e < 2:
                 pool, offset = before_w2, e * 2 * H
             else:
-                pool, offset = after_gated, 4 * PACK * (CHUNKS - EARLY) * CHUNK + (e - 2) * 2 * H
+                pool, offset = after_rounded, (e - 2) * 2 * H
             w2_code[e] = pool.tile([P, 2 * H], U8, name=f"w2_code_{e}", align_bytes=64, offset=offset)
             nc.scalar.copy(
                 w2_code[e][:].bitcast(U16).rearrange("p (t m) -> p t m", t=PACK),
@@ -156,12 +156,11 @@ def tile_moe_bdx_glu_relu_kernel(
         def to_columns(ap):
             return ap.rearrange("p (n c) t -> p n t c", c=RUN)
 
-        gated = after_gated.tile([P, PACK, GATED * CHUNK], F32, name="gated", align_bytes=64, offset=0)
-        ungated = {
-            GATED: before_w2.tile(
-                [P, PACK, (EARLY - GATED) * CHUNK], F32, name="ungated_early", align_bytes=64, offset=8 * H
-            )
-        }
+        gathered = before_w2.tile(
+            [P, 2 * PACK - 1, (GATED + 1) * CHUNK], F32, name="gathered", align_bytes=64, offset=8 * H
+        )
+        gated = gathered[:, PACK - 1 :, CHUNK:]
+        ungated = gathered[:, :PACK, : GATED * CHUNK]
 
         def gather_gated(j, first, last):
             columns = slice(first * CHUNK, last * CHUNK)
@@ -169,27 +168,27 @@ def tile_moe_bdx_glu_relu_kernel(
             nc.vector.tensor_tensor(gated[:, j, columns], planes[j][:].indirect(chosen), gates[:, columns], MULT)
 
         def gather_ungated(j, first, last):
-            base = GATED if first < EARLY else EARLY
-            place = ungated[base][:, j, (first - base) * CHUNK : (last - base) * CHUNK]
+            place = ungated[:, j, (first - GATED) * CHUNK : (last - GATED) * CHUNK]
             nc.scalar.activation(place, planes[j][:].indirect(entries(first * CHUNK, (last - first) * CHUNK)), COPY)
 
         rounded, dh, da, masked = {}, {}, {}, {}
 
         def round_gated(c):
-            rounded[c] = held.tile([P, CHUNK, PACK], BF16, name=f"rounded_{c}", align_bytes=64)
+            if c == 0:
+                rounded[c] = held.tile([P, CHUNK, PACK], BF16, name="rounded_0", align_bytes=64)
+            elif c == 1:
+                rounded[c] = after_rounded.tile([P, CHUNK, PACK], BF16, name="rounded_1", align_bytes=64, offset=0)
+            else:
+                rounded[c] = pairs.tile([P, CHUNK, PACK], BF16, name="rounded", align_bytes=64)
             nc.scalar.activation(to_columns(rounded[c][:]), from_rows(gated[:, :, c * CHUNK : (c + 1) * CHUNK]), COPY)
 
         def gate_and_round(block):
             c, b = divmod(block, BLOCKS)
             if b == 0:
-                rounded[c] = ring.tile([P, CHUNK, PACK], BF16, name="rounded_late", align_bytes=64)
+                rounded[c] = pairs.tile([P, CHUNK, PACK], BF16, name="rounded", align_bytes=64)
             e, first = divmod(block * P, C)
-            base = GATED if c < EARLY else EARLY
-            rows = ungated[base][:, :, block * P - base * CHUNK : (block + 1) * P - base * CHUNK]
-            if e in gates_in_psum:
-                factor = gates_in_psum[e][:, first // RUN : (first + P) // RUN, :]
-            else:
-                factor = gates[:, block * P : (block + 1) * P].rearrange("p (n c) -> p n c", c=RUN)
+            rows = ungated[:, :, block * P - GATED * CHUNK : (block + 1) * P - GATED * CHUNK]
+            factor = gates_in_psum[e][:, first // RUN : (first + P) // RUN, :]
             factor = factor.unsqueeze(2).broadcast_to([P, P // RUN, PACK, RUN])
             nc.vector.tensor_tensor(to_columns(rounded[c][:, b * P : (b + 1) * P, :]), from_rows(rows), factor, MULT)
 
@@ -217,15 +216,33 @@ def tile_moe_bdx_glu_relu_kernel(
                     )
 
         def mask(c):
-            masked[c] = pairs.tile([P, PACK, CHUNK], F32, name="masked", align_bytes=64)
+            if c in (0, CHUNKS - 1):
+                for b in range(BLOCKS):
+                    masked[c, b] = held.tile([P, PACK, P], F32, name=f"masked_{c}_{b}", align_bytes=64)[:]
+            else:
+                masked[c] = pairs.tile([P, PACK, CHUNK], F32, name="masked", align_bytes=64)
+                for b in range(BLOCKS):
+                    masked[c, b] = masked[c][:, :, b * P : (b + 1) * P]
             for b in range(BLOCKS):
                 nc.vector.scalar_tensor_tensor(
-                    masked[c][:, :, b * P : (b + 1) * P], saved["a1", c][:, :, b * P : (b + 1) * P], 0.0, dh[c, b][:], IS_GT, MULT
+                    masked[c, b], saved["a1", c][:, :, b * P : (b + 1) * P], 0.0, dh[c, b][:], IS_GT, MULT
                 )
+
+        def first_product(engine, c, b):
+            block = slice(b * P, (b + 1) * P)
+            engine.tensor_tensor(
+                to_columns(da[c][:, 0, block]), from_rows(masked[c, b]), from_rows(saved["a3", c][:, :, block]), MULT
+            )
 
         def products(c):
             da[c] = in_turn.tile([P, 2, CHUNK, PACK], BF16, name="da", align_bytes=64)
-            nc.gpsimd.tensor_tensor(to_columns(da[c][:, 0]), from_rows(masked[c][:]), from_rows(saved["a3", c]), MULT)
+            if c == 0:
+                for b in range(BLOCKS):
+                    first_product(nc.gpsimd, c, b)
+            elif c == CHUNKS - 1:
+                first_product(nc.gpsimd, c, 0)
+            else:
+                nc.gpsimd.tensor_tensor(to_columns(da[c][:, 0]), from_rows(masked[c][:]), from_rows(saved["a3", c]), MULT)
             for b in range(BLOCKS):
                 block = slice(b * P, (b + 1) * P)
                 nc.vector.scalar_tensor_tensor(
@@ -236,6 +253,8 @@ def tile_moe_bdx_glu_relu_kernel(
                     MAX,
                     MULT,
                 )
+            if c == CHUNKS - 1:
+                first_product(nc.vector, c, 1)
 
         windows = [held.tile([P, T], F32, name=f"window_{k}") for k in range(K_BLOCKS)]
 
@@ -262,9 +281,9 @@ def tile_moe_bdx_glu_relu_kernel(
                     copy(dx[:, k, :], bank[:, k, :])
             if not last:
                 nc.scalar.copy(dx[:], bank[:])
-            for k in range(K_BLOCKS):
+            for k in reversed(range(K_BLOCKS)):
                 place = windows[k][:].indirect(entries(c * CHUNK, CHUNK))
-                if c >= CHUNKS - 2 and k:
+                if last and k:
                     nc.vector.tensor_copy(place, dx[:, k, :])
                 else:
                     nc.scalar.activation(place, dx[:, k, :], COPY)
@@ -273,30 +292,26 @@ def tile_moe_bdx_glu_relu_kernel(
         permute_w2(1)
         for j in range(PACK - 1):
             gather_gated(j, 0, GATED)
-            gather_ungated(j, GATED, EARLY)
+            gather_ungated(j, GATED, CHUNKS)
         for c in range(GATED):
             gather_gated(PACK - 1, c, c + 1)
         gather_ungated(PACK - 1, GATED, GATED + 1)
         round_gated(0)
         round_gated(1)
-        gather_ungated(PACK - 1, GATED + 1, EARLY)
+        gather_ungated(PACK - 1, GATED + 1, GATED + 2)
         round_gated(2)
-        ungated[EARLY] = after_gated.tile(
-            [P, PACK, (CHUNKS - EARLY) * CHUNK], F32, name="ungated_late", align_bytes=64, offset=0
-        )
-        for j in range(PACK):
-            gather_ungated(j, EARLY, CHUNKS)
+        gather_ungated(PACK - 1, GATED + 2, GATED + 3)
+        hidden_gradient(0)
+        hidden_gradient(1)
+        round_gated(3)
+        gather_ungated(PACK - 1, GATED + 3, CHUNKS)
         permute_w2(2)
         permute_w2(3)
         blocks = list(range(GATED * BLOCKS, CHUNKS * BLOCKS))
-        hidden_gradient(0)
-        gate_and_round(blocks.pop(0))
-        hidden_gradient(1)
-        gate_and_round(blocks.pop(0))
         mask(0)
         for c in range(CHUNKS):
             products(c)
-            for block in blocks[: 2 if c < 2 else 1]:
+            for block in blocks[: (c + 1) // 2 if c < 3 else 2]:
                 gate_and_round(blocks.pop(0))
             if c + 1 < CHUNKS:
                 mask(c + 1)

@@ -43,6 +43,7 @@ def tile_moe_bdx_glu_relu_kernel(
         before_w2 = ctx.enter_context(tc.tile_pool(name="before_w2", bufs=1))
         after_rounded = ctx.enter_context(tc.tile_pool(name="after_rounded", bufs=1))
         pairs = ctx.enter_context(tc.tile_pool(name="pairs", bufs=2))
+        two_places = ctx.enter_context(tc.tile_pool(name="two_places", bufs=1))
         in_turn = ctx.enter_context(tc.tile_pool(name="in_turn", bufs=1))
         dh_banks = ctx.enter_context(tc.psum_pool(name="dh_banks", bufs=2 * BLOCKS))
         dx_banks = ctx.enter_context(tc.psum_pool(name="dx_banks", bufs=2))
@@ -104,24 +105,32 @@ def tile_moe_bdx_glu_relu_kernel(
         load_plane(1)
         load_plane(2)
         load_plane(3)
-        load_gates(2, held.tile([P, 2, 2 * PACK], F32, name="gate_columns_late"))
+        late = held.tile([P, 2, PACK], F32, name="gate_columns_late")
+        nc.sync.dma_start(late[:], gate[0, 2 * C :].rearrange("(e c p) -> p e c", e=2, c=PACK))
+        gate_columns[2], gate_columns[3] = late[:, 0], late[:, 1]
         load_saved("a1", a1, 0, CHUNK)
-        w2_raw[2] = load_words("w2_raw_2", w2_words, 2, E)
-        load_saved("a3", a3, 0, CHUNK)
         load_saved("a1", a1, CHUNK, CHUNK)
+        load_saved("a3", a3, 0, CHUNK)
+        w2_raw[2] = load_words("w2_raw_2", w2_words, 2, E)
+        load_scales(w1_scale, w1_scales)
         w1_code = load_words("w1_code", w1_words, 0, E)
         w3_code = load_words("w3_code", w3_words, 0, E)
-        load_scales(w1_scale, w1_scales)
         load_scales(w3_scale, w3_scales)
-        load_saved("a3", a3, CHUNK, CHUNK)
-        for e in range(1, E):
-            load_saved("a1", a1, e * C, C)
-            load_saved("a3", a3, e * C, C)
+        for c in (1, 2):
+            load_saved("a1", a1, (c + 1) * CHUNK, CHUNK)
+            load_saved("a3", a3, c * CHUNK, CHUNK)
+        load_saved("a1", a1, 2 * C, C)
+        load_saved("a3", a3, 3 * CHUNK, CHUNK)
+        load_saved("a1", a1, 3 * C, C)
+        load_saved("a3", a3, 2 * C, C)
+        load_saved("a3", a3, 3 * C, C)
 
         def spread_gates(e, pool, name):
             bank = pool.tile([P, PACK, P], F32, name=name)
             for c in range(PACK):
                 nc.tensor.transpose(bank[:, c, :], gate_columns[e][:, c : c + 1].to_broadcast([P, P]), identity[:])
+            if e >= 2:
+                return bank[:].rearrange("p c (n r) -> p (c n) r", r=RUN)
             return bank[:].rearrange("p c n -> p n c")
 
         gates = held.tile([P, 2 * C], F32, name="gates")
@@ -192,15 +201,23 @@ def tile_moe_bdx_glu_relu_kernel(
             factor = factor.unsqueeze(2).broadcast_to([P, P // RUN, PACK, RUN])
             nc.vector.tensor_tensor(to_columns(rounded[c][:, b * P : (b + 1) * P, :]), from_rows(rows), factor, MULT)
 
-        def quantise(values, columns, name):
+        def masked_bytes(c, b):
+            return 4 * PACK * (c % 2 * CHUNK + b * P)
+
+        def quantise(values, columns, name, scale=None):
             code = ring.tile([P, columns], U32, name=name + "_code", align_bytes=64)
-            scale = ring.tile([P, columns], U8, name=name + "_scale", align_bytes=64)
+            if scale is None:
+                scale = ring.tile([P, columns], U8, name=name + "_scale", align_bytes=64)
             nc.vector.quantize_mx(out=code[:].bitcast(E5M2X4), scales=scale[:], in_=values)
             return code, scale
 
         def hidden_gradient(c):
             e = c * CHUNK // C
-            code, scale = quantise(rounded[c][:].rearrange("p c t -> p (c t)"), CHUNK, "g")
+            scale = None
+            if c >= 2:
+                offset = masked_bytes(c, 1)
+                scale = two_places.tile([P, CHUNK], U8, name=f"g_scale_{c}", align_bytes=64, offset=offset)
+            code, scale = quantise(rounded[c][:].rearrange("p c t -> p (c t)"), CHUNK, "g", scale)
             for b in range(BLOCKS):
                 block = slice(b * P, (b + 1) * P)
                 bank = dh[c, b] = dh_banks.tile([P, PACK, P], F32, name="dh")
@@ -218,9 +235,11 @@ def tile_moe_bdx_glu_relu_kernel(
         def mask(c):
             if c in (0, CHUNKS - 1):
                 for b in range(BLOCKS):
-                    masked[c, b] = held.tile([P, PACK, P], F32, name=f"masked_{c}_{b}", align_bytes=64)[:]
+                    offset = masked_bytes(c, b)
+                    masked[c, b] = two_places.tile([P, PACK, P], F32, name=f"masked_{c}_{b}", align_bytes=64, offset=offset)[:]
             else:
-                masked[c] = pairs.tile([P, PACK, CHUNK], F32, name="masked", align_bytes=64)
+                offset = masked_bytes(c, 0)
+                masked[c] = two_places.tile([P, PACK, CHUNK], F32, name=f"masked_{c}", align_bytes=64, offset=offset)
                 for b in range(BLOCKS):
                     masked[c, b] = masked[c][:, :, b * P : (b + 1) * P]
             for b in range(BLOCKS):
@@ -315,8 +334,8 @@ def tile_moe_bdx_glu_relu_kernel(
                 gate_and_round(blocks.pop(0))
             if c + 1 < CHUNKS:
                 mask(c + 1)
-            input_gradient(c)
             if c + 2 < CHUNKS:
                 hidden_gradient(c + 2)
+            input_gradient(c)
         for k, queue in enumerate((nc.scalar, nc.sync)):
             queue.dma_start(out[k * P : (k + 1) * P, :], windows[k][:])

@@ -30,6 +30,7 @@ E2M1X4 = mybir.dt.float4_e2m1fn_x4
 MULT = mybir.AluOpType.mult
 MAX = mybir.AluOpType.max
 IS_GT = mybir.AluOpType.is_gt
+RELU = mybir.ActivationFunctionType.Relu
 COPY = mybir.ActivationFunctionType.Copy
 
 
@@ -166,9 +167,10 @@ def tile_moe_bdx_glu_relu_kernel(
             return ap.rearrange("p (n c) t -> p n t c", c=RUN)
 
         gathered = before_w2.tile(
-            [P, 2 * PACK - 1, (GATED + 1) * CHUNK], F32, name="gathered", align_bytes=64, offset=8 * H
+            [P, 2 * PACK, (GATED + 1) * CHUNK], F32, name="gathered", align_bytes=64, offset=8 * H
         )
-        gated = gathered[:, PACK - 1 :, CHUNK:]
+        gated = gathered[:, PACK - 1 : 2 * PACK - 1, CHUNK:]
+        spent = gathered[:, PACK:, CHUNK:]
         ungated = gathered[:, :PACK, : GATED * CHUNK]
 
         def gather_gated(j, first, last):
@@ -247,6 +249,12 @@ def tile_moe_bdx_glu_relu_kernel(
                     masked[c, b], saved["a1", c][:, :, b * P : (b + 1) * P], 0.0, dh[c, b][:], IS_GT, MULT
                 )
 
+        positive = {}
+
+        def relu(c, column):
+            positive[c] = spent[:, :, column : column + CHUNK]
+            nc.scalar.activation(positive[c], saved["a1", c], RELU)
+
         def first_product(engine, c, b):
             block = slice(b * P, (b + 1) * P)
             engine.tensor_tensor(
@@ -264,6 +272,11 @@ def tile_moe_bdx_glu_relu_kernel(
                 nc.gpsimd.tensor_tensor(to_columns(da[c][:, 0]), from_rows(masked[c][:]), from_rows(saved["a3", c]), MULT)
             for b in range(BLOCKS):
                 block = slice(b * P, (b + 1) * P)
+                if c in positive:
+                    nc.vector.tensor_tensor(
+                        to_columns(da[c][:, 1, block, :]), from_rows(dh[c, b][:]), from_rows(positive[c][:, :, block]), MULT
+                    )
+                    continue
                 nc.vector.scalar_tensor_tensor(
                     da[c][:, 1, block, :],
                     saved["a1", c][:, :, block].rearrange("p t c -> p c t"),
@@ -319,6 +332,7 @@ def tile_moe_bdx_glu_relu_kernel(
         round_gated(1)
         gather_ungated(PACK - 1, GATED + 1, GATED + 2)
         round_gated(2)
+        relu(1, CHUNK)
         gather_ungated(PACK - 1, GATED + 2, GATED + 3)
         hidden_gradient(0)
         hidden_gradient(1)
@@ -326,6 +340,7 @@ def tile_moe_bdx_glu_relu_kernel(
         gather_ungated(PACK - 1, GATED + 3, CHUNKS)
         permute_w2(2)
         permute_w2(3)
+        relu(2, 0)
         blocks = list(range(GATED * BLOCKS, CHUNKS * BLOCKS))
         mask(0)
         for c in range(CHUNKS):

@@ -30,7 +30,6 @@ E2M1X4 = mybir.dt.float4_e2m1fn_x4
 MULT = mybir.AluOpType.mult
 MAX = mybir.AluOpType.max
 IS_GT = mybir.AluOpType.is_gt
-RELU = mybir.ActivationFunctionType.Relu
 COPY = mybir.ActivationFunctionType.Copy
 
 
@@ -41,11 +40,11 @@ def tile_moe_bdx_glu_relu_kernel(
     with ExitStack() as ctx:
         held = ctx.enter_context(tc.tile_pool(name="held", bufs=1))
         ring = ctx.enter_context(tc.tile_pool(name="ring", bufs=3))
-        before_w2 = ctx.enter_context(tc.tile_pool(name="before_w2", bufs=1))
-        after_rounded = ctx.enter_context(tc.tile_pool(name="after_rounded", bufs=1))
-        pairs = ctx.enter_context(tc.tile_pool(name="pairs", bufs=2))
+        joints = ctx.enter_context(tc.tile_pool(name="joints", bufs=4))
+        after_gates = ctx.enter_context(tc.tile_pool(name="after_gates", bufs=1))
+        after_first = ctx.enter_context(tc.tile_pool(name="after_first", bufs=1))
+        after_plane = ctx.enter_context(tc.tile_pool(name="after_plane", bufs=1))
         two_places = ctx.enter_context(tc.tile_pool(name="two_places", bufs=1))
-        in_turn = ctx.enter_context(tc.tile_pool(name="in_turn", bufs=1))
         dh_banks = ctx.enter_context(tc.psum_pool(name="dh_banks", bufs=2 * BLOCKS))
         dx_banks = ctx.enter_context(tc.psum_pool(name="dx_banks", bufs=2))
         gate_banks = ctx.enter_context(tc.psum_pool(name="gate_banks", bufs=2))
@@ -76,20 +75,17 @@ def tile_moe_bdx_glu_relu_kernel(
         for tile in (w1_scale, w3_scale):
             nc.gpsimd.memset(tile[:].bitcast(I32), 0)
 
-        gate_columns = {}
-
-        def load_gates(first, tile):
-            row = gate[0, first * C : (first + 2) * C]
-            nc.sync.dma_start(tile[:, :, 0:PACK], row.rearrange("(e p c) -> p e c", e=2, c=PACK))
-            gate_columns[first], gate_columns[first + 1] = tile[:, 0], tile[:, 1]
-
-        load_gates(0, before_w2.tile([P, 2, H + 8], F32, name="gate_columns", align_bytes=64, offset=0))
-        load_scales(w2_scale_raw, w2_scales)
+        early = after_gates.tile([P, 2, 2 * PACK], F32, name="gate_columns", align_bytes=64, offset=0)
+        nc.sync.dma_start(early[:, :, 0:PACK], gate[0, : 2 * C].rearrange("(e p c) -> p e c", e=2, c=PACK))
+        gate_columns = {0: early[:, 0], 1: early[:, 1]}
 
         planes = {}
 
         def load_plane(j):
-            planes[j] = held.tile([P, T], F32, name=f"plane_{j}")
+            if j == 0:
+                planes[j] = after_plane.tile([P, T], F32, name="plane_0", align_bytes=64, offset=0)
+            else:
+                planes[j] = held.tile([P, T], F32, name=f"plane_{j}")
             nc.sync.dma_start(planes[j][:], dyT.rearrange("(p j) s -> p j s", j=PACK)[:, j, :])
 
         saved = {}
@@ -100,38 +96,45 @@ def tile_moe_bdx_glu_relu_kernel(
             for c in range(count // CHUNK):
                 saved[name, first // CHUNK + c] = tile[:, :, c * CHUNK : (c + 1) * CHUNK]
 
-        w2_raw = {0: load_words("w2_raw_0", w2_words, 0, 2)}
+        w2_raw = {}
+
+        def load_w2(e):
+            w2_raw[e] = held.tile([P, 2 * H], U8, name=f"w2_raw_{e}", align_bytes=64)
+            nc.sync.dma_start(w2_raw[e][:].bitcast(I32), w2_words[e, 0].bitcast(I32))
+
         load_plane(0)
         nc.sync.dma_start(offsets[:], offs)
         load_plane(1)
+        load_w2(0)
+        load_scales(w2_scale_raw, w2_scales)
+        late = held.tile([P, 2, 2 * PACK], F32, name="gate_columns_late")
+        nc.sync.dma_start(late[:, :, 0:PACK], gate[0, 2 * C :].rearrange("(e p c) -> p e c", e=2, c=PACK))
+        gate_columns[2], gate_columns[3] = late[:, 0], late[:, 1]
         load_plane(2)
         load_plane(3)
-        late = held.tile([P, 2, PACK], F32, name="gate_columns_late")
-        nc.sync.dma_start(late[:], gate[0, 2 * C :].rearrange("(e c p) -> p e c", e=2, c=PACK))
-        gate_columns[2], gate_columns[3] = late[:, 0], late[:, 1]
         load_saved("a1", a1, 0, CHUNK)
-        load_saved("a1", a1, CHUNK, CHUNK)
         load_saved("a3", a3, 0, CHUNK)
-        w2_raw[2] = load_words("w2_raw_2", w2_words, 2, E)
+        load_saved("a1", a1, CHUNK, CHUNK)
+        load_w2(1)
         load_scales(w1_scale, w1_scales)
         w1_code = load_words("w1_code", w1_words, 0, E)
         w3_code = load_words("w3_code", w3_words, 0, E)
         load_scales(w3_scale, w3_scales)
-        for c in (1, 2):
-            load_saved("a1", a1, (c + 1) * CHUNK, CHUNK)
-            load_saved("a3", a3, c * CHUNK, CHUNK)
-        load_saved("a1", a1, 2 * C, C)
+        load_saved("a3", a3, CHUNK, CHUNK)
+        load_saved("a1", a1, 2 * CHUNK, CHUNK)
+        load_w2(2)
+        load_saved("a3", a3, 2 * CHUNK, CHUNK)
+        load_saved("a1", a1, 3 * CHUNK, CHUNK)
         load_saved("a3", a3, 3 * CHUNK, CHUNK)
-        load_saved("a1", a1, 3 * C, C)
-        load_saved("a3", a3, 2 * C, C)
-        load_saved("a3", a3, 3 * C, C)
+        load_w2(3)
+        for e in (2, 3):
+            load_saved("a1", a1, e * C, C)
+            load_saved("a3", a3, e * C, C)
 
         def spread_gates(e, pool, name):
             bank = pool.tile([P, PACK, P], F32, name=name)
             for c in range(PACK):
                 nc.tensor.transpose(bank[:, c, :], gate_columns[e][:, c : c + 1].to_broadcast([P, P]), identity[:])
-            if e >= 2:
-                return bank[:].rearrange("p c (n r) -> p (c n) r", r=RUN)
             return bank[:].rearrange("p c n -> p n c")
 
         gates = held.tile([P, 2 * C], F32, name="gates")
@@ -143,21 +146,23 @@ def tile_moe_bdx_glu_relu_kernel(
                 nc.scalar.activation(place, spread_gates(e, dx_banks, "dx"), COPY)
         gates_in_psum = {e: spread_gates(e, gate_banks, "gate_bank") for e in range(2, E)}
 
-        w2_scale = before_w2.tile([P, E, H], U8, name="w2_scale", align_bytes=64, offset=4 * H)
-        nc.vector.tensor_copy(
-            w2_scale[:].rearrange("p e (t m) -> p e t m", t=PACK), w2_scale_raw[:].rearrange("p e (m t) -> p e t m", t=PACK)
-        )
+        w2_scale = after_plane.tile([P, E, H], U8, name="w2_scale", align_bytes=64, offset=0)
         w2_code = {}
 
+        def permute_w2_scale():
+            nc.vector.tensor_copy(
+                w2_scale[:].rearrange("p e (t m) -> p e t m", t=PACK),
+                w2_scale_raw[:].rearrange("p e (m t) -> p e t m", t=PACK),
+            )
+
         def permute_w2(e):
-            if e < 2:
-                pool, offset = before_w2, e * 2 * H
+            if e == 0:
+                w2_code[e] = after_plane.tile([P, 2 * H], U8, name="w2_code_0", align_bytes=64, offset=E * H)
             else:
-                pool, offset = after_rounded, (e - 2) * 2 * H
-            w2_code[e] = pool.tile([P, 2 * H], U8, name=f"w2_code_{e}", align_bytes=64, offset=offset)
+                w2_code[e] = after_first.tile([P, 2 * H], U8, name=f"w2_code_{e}", align_bytes=64, offset=2 * H * e)
             nc.scalar.copy(
                 w2_code[e][:].bitcast(U16).rearrange("p (t m) -> p t m", t=PACK),
-                w2_raw[e - e % 2][:, e % 2, :].bitcast(U16).rearrange("p (m t) -> p t m", t=PACK),
+                w2_raw[e][:].bitcast(U16).rearrange("p (m t) -> p t m", t=PACK),
             )
 
         def from_rows(ap):
@@ -166,12 +171,9 @@ def tile_moe_bdx_glu_relu_kernel(
         def to_columns(ap):
             return ap.rearrange("p (n c) t -> p n t c", c=RUN)
 
-        gathered = before_w2.tile(
-            [P, 2 * PACK, (GATED + 1) * CHUNK], F32, name="gathered", align_bytes=64, offset=8 * H
-        )
-        gated = gathered[:, PACK - 1 : 2 * PACK - 1, CHUNK:]
-        spent = gathered[:, PACK:, CHUNK:]
-        ungated = gathered[:, :PACK, : GATED * CHUNK]
+        gathered = after_gates.tile([P, 2 * PACK - 1, GATED * CHUNK], F32, name="gathered", align_bytes=64, offset=0)
+        gated = gathered[:, PACK - 1 :, :]
+        ungated = gathered[:, :PACK, :]
 
         def gather_gated(j, first, last):
             columns = slice(first * CHUNK, last * CHUNK)
@@ -184,19 +186,29 @@ def tile_moe_bdx_glu_relu_kernel(
 
         rounded, dh, da, masked = {}, {}, {}, {}
 
-        def round_gated(c):
+        def place_rounded(c):
             if c == 0:
-                rounded[c] = held.tile([P, CHUNK, PACK], BF16, name="rounded_0", align_bytes=64)
-            elif c == 1:
-                rounded[c] = after_rounded.tile([P, CHUNK, PACK], BF16, name="rounded_1", align_bytes=64, offset=0)
+                rounded[c] = after_first.tile([P, CHUNK, PACK], BF16, name="rounded_0", align_bytes=64, offset=0)[:]
+                return
+            if c == CHUNKS - 1:
+                tile = held.tile([P, 3, CHUNK, PACK], BF16, name="last_joint", align_bytes=64)
+                da[c] = tile[:, 1:3]
             else:
-                rounded[c] = pairs.tile([P, CHUNK, PACK], BF16, name="rounded", align_bytes=64)
-            nc.scalar.activation(to_columns(rounded[c][:]), from_rows(gated[:, :, c * CHUNK : (c + 1) * CHUNK]), COPY)
+                tile = joints.tile([P, 2, CHUNK, PACK], BF16, name="joint", align_bytes=64)
+            da[c - 1] = tile[:, 0:2]
+            rounded[c] = tile[:, 0]
+
+        def round_gated(c, pieces=1):
+            place_rounded(c)
+            width = CHUNK // pieces
+            for first in range(0, CHUNK, width):
+                rows = gated[:, :, c * CHUNK + first : c * CHUNK + first + width]
+                nc.scalar.activation(to_columns(rounded[c][:, first : first + width, :]), from_rows(rows), COPY)
 
         def gate_and_round(block):
             c, b = divmod(block, BLOCKS)
             if b == 0:
-                rounded[c] = pairs.tile([P, CHUNK, PACK], BF16, name="rounded", align_bytes=64)
+                place_rounded(c)
             e, first = divmod(block * P, C)
             rows = ungated[:, :, block * P - GATED * CHUNK : (block + 1) * P - GATED * CHUNK]
             factor = gates_in_psum[e][:, first // RUN : (first + P) // RUN, :]
@@ -206,22 +218,23 @@ def tile_moe_bdx_glu_relu_kernel(
         def masked_bytes(c, b):
             return 4 * PACK * (c % 2 * CHUNK + b * P)
 
-        def quantise(values, columns, name, scale=None):
-            code = ring.tile([P, columns], U32, name=name + "_code", align_bytes=64)
-            if scale is None:
-                scale = ring.tile([P, columns], U8, name=name + "_scale", align_bytes=64)
-            nc.vector.quantize_mx(out=code[:].bitcast(E5M2X4), scales=scale[:], in_=values)
-            return code, scale
+        def quantise(values, code, scale):
+            nc.vector.quantize_mx(out=code.bitcast(E5M2X4), scales=scale, in_=values)
 
-        def hidden_gradient(c):
+        def hidden_gradient(c, pieces=1):
             e = c * CHUNK // C
-            scale = None
+            code = ring.tile([P, CHUNK], U32, name="g_code", align_bytes=64)
             if c >= 2:
                 offset = masked_bytes(c, 1)
                 scale = two_places.tile([P, CHUNK], U8, name=f"g_scale_{c}", align_bytes=64, offset=offset)
-            code, scale = quantise(rounded[c][:].rearrange("p c t -> p (c t)"), CHUNK, "g", scale)
+            else:
+                scale = ring.tile([P, CHUNK], U8, name="g_scale", align_bytes=64)
+            width = CHUNK // pieces
             for b in range(BLOCKS):
                 block = slice(b * P, (b + 1) * P)
+                if b * P % width == 0:
+                    piece = slice(b * P, b * P + width)
+                    quantise(rounded[c][:, piece, :].rearrange("p c t -> p (c t)"), code[:, piece], scale[:, piece])
                 bank = dh[c, b] = dh_banks.tile([P, PACK, P], F32, name="dh")
                 for t in range(PACK):
                     nc.tensor.matmul_mx(
@@ -249,12 +262,6 @@ def tile_moe_bdx_glu_relu_kernel(
                     masked[c, b], saved["a1", c][:, :, b * P : (b + 1) * P], 0.0, dh[c, b][:], IS_GT, MULT
                 )
 
-        positive = {}
-
-        def relu(c, column):
-            positive[c] = spent[:, :, column : column + CHUNK]
-            nc.scalar.activation(positive[c], saved["a1", c], RELU)
-
         def first_product(engine, c, b):
             block = slice(b * P, (b + 1) * P)
             engine.tensor_tensor(
@@ -262,7 +269,6 @@ def tile_moe_bdx_glu_relu_kernel(
             )
 
         def products(c):
-            da[c] = in_turn.tile([P, 2, CHUNK, PACK], BF16, name="da", align_bytes=64)
             if c == 0:
                 for b in range(BLOCKS):
                     first_product(nc.gpsimd, c, b)
@@ -272,11 +278,6 @@ def tile_moe_bdx_glu_relu_kernel(
                 nc.gpsimd.tensor_tensor(to_columns(da[c][:, 0]), from_rows(masked[c][:]), from_rows(saved["a3", c]), MULT)
             for b in range(BLOCKS):
                 block = slice(b * P, (b + 1) * P)
-                if c in positive:
-                    nc.vector.tensor_tensor(
-                        to_columns(da[c][:, 1, block, :]), from_rows(dh[c, b][:]), from_rows(positive[c][:, :, block]), MULT
-                    )
-                    continue
                 nc.vector.scalar_tensor_tensor(
                     da[c][:, 1, block, :],
                     saved["a1", c][:, :, block].rearrange("p t c -> p c t"),
@@ -293,10 +294,15 @@ def tile_moe_bdx_glu_relu_kernel(
         def input_gradient(c):
             e = c * CHUNK // C
             last = c == CHUNKS - 1
-            code, scale = quantise(da[c][:].rearrange("p a c t -> p (a c t)"), 2 * CHUNK, "da")
+            if c == 0:
+                code = after_first.tile([P, 2 * CHUNK], U32, name="da_code_0", align_bytes=64, offset=4 * H)
+            else:
+                code = ring.tile([P, 2 * CHUNK], U32, name="da_code", align_bytes=64)
+            scale = ring.tile([P, 2 * CHUNK], U8, name="da_scale", align_bytes=64)
+            quantise(da[c].rearrange("p a c t -> p (a c t)"), code[:], scale[:])
             dx = ring.tile([P, K_BLOCKS, CHUNK], F32, name="dx_out")
-            for k in range(K_BLOCKS):
-                if k == 0 or last:
+            for k in reversed(range(K_BLOCKS)):
+                if k == K_BLOCKS - 1 or last:
                     bank = dx_banks.tile([P, K_BLOCKS, CHUNK], F32, name="dx")
                 for a, (w_code, w_scale) in enumerate(((w1_code, w1_scale), (w3_code, w3_scale))):
                     nc.tensor.matmul_mx(
@@ -320,37 +326,37 @@ def tile_moe_bdx_glu_relu_kernel(
                 else:
                     nc.scalar.activation(place, dx[:, k, :], COPY)
 
-        permute_w2(0)
-        permute_w2(1)
         for j in range(PACK - 1):
             gather_gated(j, 0, GATED)
             gather_ungated(j, GATED, CHUNKS)
+            if j == 1:
+                permute_w2(0)
+                permute_w2_scale()
         for c in range(GATED):
             gather_gated(PACK - 1, c, c + 1)
-        gather_ungated(PACK - 1, GATED, GATED + 1)
-        round_gated(0)
+        round_gated(0, BLOCKS)
         round_gated(1)
-        gather_ungated(PACK - 1, GATED + 1, GATED + 2)
-        round_gated(2)
-        relu(1, CHUNK)
-        gather_ungated(PACK - 1, GATED + 2, GATED + 3)
-        hidden_gradient(0)
+        hidden_gradient(0, BLOCKS)
         hidden_gradient(1)
-        round_gated(3)
-        gather_ungated(PACK - 1, GATED + 3, CHUNKS)
-        permute_w2(2)
-        permute_w2(3)
-        relu(2, 0)
-        blocks = list(range(GATED * BLOCKS, CHUNKS * BLOCKS))
         mask(0)
+        gather_ungated(PACK - 1, GATED, GATED + 1)
+        round_gated(2)
+        permute_w2(1)
+        gather_ungated(PACK - 1, GATED + 1, GATED + 2)
+        round_gated(3)
+        gather_ungated(PACK - 1, GATED + 2, GATED + 3)
+        gather_ungated(PACK - 1, GATED + 3, CHUNKS)
+        blocks = list(range(GATED * BLOCKS, CHUNKS * BLOCKS))
         for c in range(CHUNKS):
             products(c)
-            for block in blocks[: (c + 1) // 2 if c < 3 else 2]:
+            for block in blocks[: (1, 1, 2, 2, 1, 1, 0, 0)[c]]:
                 gate_and_round(blocks.pop(0))
             if c + 1 < CHUNKS:
                 mask(c + 1)
             if c + 2 < CHUNKS:
                 hidden_gradient(c + 2)
             input_gradient(c)
+            if c < 2:
+                permute_w2(c + 2)
         for k, queue in enumerate((nc.scalar, nc.sync)):
             queue.dma_start(out[k * P : (k + 1) * P, :], windows[k][:])

@@ -40,7 +40,7 @@ def tile_moe_bdx_glu_relu_kernel(
     with ExitStack() as ctx:
         held = ctx.enter_context(tc.tile_pool(name="held", bufs=1))
         ring = ctx.enter_context(tc.tile_pool(name="ring", bufs=3))
-        joints = ctx.enter_context(tc.tile_pool(name="joints", bufs=4))
+        joints = ctx.enter_context(tc.tile_pool(name="joints", bufs=1))
         after_gates = ctx.enter_context(tc.tile_pool(name="after_gates", bufs=1))
         after_first = ctx.enter_context(tc.tile_pool(name="after_first", bufs=1))
         after_plane = ctx.enter_context(tc.tile_pool(name="after_plane", bufs=1))
@@ -78,12 +78,14 @@ def tile_moe_bdx_glu_relu_kernel(
         early = after_gates.tile([P, 2, 2 * PACK], F32, name="gate_columns", align_bytes=64, offset=0)
         nc.sync.dma_start(early[:, :, 0:PACK], gate[0, : 2 * C].rearrange("(e p c) -> p e c", e=2, c=PACK))
         gate_columns = {0: early[:, 0], 1: early[:, 1]}
+        nc.sync.dma_start(offsets[:], offs)
+        load_scales(w2_scale_raw, w2_scales)
 
         planes = {}
 
         def load_plane(j):
-            if j == 0:
-                planes[j] = after_plane.tile([P, T], F32, name="plane_0", align_bytes=64, offset=0)
+            if j == 2:
+                planes[j] = after_plane.tile([P, T], F32, name="plane_2", align_bytes=64, offset=0)
             else:
                 planes[j] = held.tile([P, T], F32, name=f"plane_{j}")
             nc.sync.dma_start(planes[j][:], dyT.rearrange("(p j) s -> p j s", j=PACK)[:, j, :])
@@ -103,10 +105,8 @@ def tile_moe_bdx_glu_relu_kernel(
             nc.sync.dma_start(w2_raw[e][:].bitcast(I32), w2_words[e, 0].bitcast(I32))
 
         load_plane(0)
-        nc.sync.dma_start(offsets[:], offs)
         load_plane(1)
         load_w2(0)
-        load_scales(w2_scale_raw, w2_scales)
         late = held.tile([P, 2, 2 * PACK], F32, name="gate_columns_late")
         nc.sync.dma_start(late[:, :, 0:PACK], gate[0, 2 * C :].rearrange("(e p c) -> p e c", e=2, c=PACK))
         gate_columns[2], gate_columns[3] = late[:, 0], late[:, 1]
@@ -121,12 +121,12 @@ def tile_moe_bdx_glu_relu_kernel(
         w3_code = load_words("w3_code", w3_words, 0, E)
         load_scales(w3_scale, w3_scales)
         load_saved("a3", a3, CHUNK, CHUNK)
-        load_saved("a1", a1, 2 * CHUNK, CHUNK)
         load_w2(2)
+        load_w2(3)
+        load_saved("a1", a1, 2 * CHUNK, CHUNK)
         load_saved("a3", a3, 2 * CHUNK, CHUNK)
         load_saved("a1", a1, 3 * CHUNK, CHUNK)
         load_saved("a3", a3, 3 * CHUNK, CHUNK)
-        load_w2(3)
         for e in (2, 3):
             load_saved("a1", a1, e * C, C)
             load_saved("a3", a3, e * C, C)
@@ -146,7 +146,7 @@ def tile_moe_bdx_glu_relu_kernel(
                 nc.scalar.activation(place, spread_gates(e, dx_banks, "dx"), COPY)
         gates_in_psum = {e: spread_gates(e, gate_banks, "gate_bank") for e in range(2, E)}
 
-        w2_scale = after_plane.tile([P, E, H], U8, name="w2_scale", align_bytes=64, offset=0)
+        w2_scale = held.tile([P, E, H], U8, name="w2_scale", align_bytes=64)
         w2_code = {}
 
         def permute_w2_scale():
@@ -157,7 +157,7 @@ def tile_moe_bdx_glu_relu_kernel(
 
         def permute_w2(e):
             if e == 0:
-                w2_code[e] = after_plane.tile([P, 2 * H], U8, name="w2_code_0", align_bytes=64, offset=E * H)
+                w2_code[e] = after_plane.tile([P, 2 * H], U8, name="w2_code_0", align_bytes=64, offset=0)
             else:
                 w2_code[e] = after_first.tile([P, 2 * H], U8, name=f"w2_code_{e}", align_bytes=64, offset=2 * H * e)
             nc.scalar.copy(
@@ -171,7 +171,9 @@ def tile_moe_bdx_glu_relu_kernel(
         def to_columns(ap):
             return ap.rearrange("p (n c) t -> p n t c", c=RUN)
 
-        gathered = after_gates.tile([P, 2 * PACK - 1, GATED * CHUNK], F32, name="gathered", align_bytes=64, offset=0)
+        row = GATED * CHUNK
+        flat = after_gates.tile([P, (2 * PACK - 1) * row], F32, name="gathered", align_bytes=64, offset=0)
+        gathered = flat[:].rearrange("p (r s) -> p r s", s=row)
         gated = gathered[:, PACK - 1 :, :]
         ungated = gathered[:, :PACK, :]
 
@@ -188,22 +190,26 @@ def tile_moe_bdx_glu_relu_kernel(
 
         def place_rounded(c):
             if c == 0:
-                rounded[c] = after_first.tile([P, CHUNK, PACK], BF16, name="rounded_0", align_bytes=64, offset=0)[:]
+                rounded[c, 0] = flat[:, -CHUNK:].bitcast(BF16).rearrange("p (c t) -> p c t", t=PACK)
+                rounded[c, 1] = after_first.tile([P, P, PACK], BF16, name="rounded_0", align_bytes=64, offset=6 * H)[:]
                 return
+            offset = (c - 1 if c <= GATED else c - GATED) * 4 * CHUNK * PACK
+            halves = 3 if c == CHUNKS - 1 else 2
+            tile = joints.tile([P, halves, CHUNK, PACK], BF16, name=f"joint_{c}", align_bytes=64, offset=offset)
             if c == CHUNKS - 1:
-                tile = held.tile([P, 3, CHUNK, PACK], BF16, name="last_joint", align_bytes=64)
                 da[c] = tile[:, 1:3]
-            else:
-                tile = joints.tile([P, 2, CHUNK, PACK], BF16, name="joint", align_bytes=64)
             da[c - 1] = tile[:, 0:2]
             rounded[c] = tile[:, 0]
+            for b in range(BLOCKS):
+                rounded[c, b] = tile[:, 0, b * P : (b + 1) * P, :]
 
-        def round_gated(c, pieces=1):
+        def round_gated(c):
             place_rounded(c)
-            width = CHUNK // pieces
-            for first in range(0, CHUNK, width):
-                rows = gated[:, :, c * CHUNK + first : c * CHUNK + first + width]
-                nc.scalar.activation(to_columns(rounded[c][:, first : first + width, :]), from_rows(rows), COPY)
+            if c > 0:
+                nc.scalar.activation(to_columns(rounded[c]), from_rows(gated[:, :, c * CHUNK : (c + 1) * CHUNK]), COPY)
+                return
+            for b in range(BLOCKS):
+                nc.scalar.activation(to_columns(rounded[c, b]), from_rows(gated[:, :, b * P : (b + 1) * P]), COPY)
 
         def gate_and_round(block):
             c, b = divmod(block, BLOCKS)
@@ -213,7 +219,7 @@ def tile_moe_bdx_glu_relu_kernel(
             rows = ungated[:, :, block * P - GATED * CHUNK : (block + 1) * P - GATED * CHUNK]
             factor = gates_in_psum[e][:, first // RUN : (first + P) // RUN, :]
             factor = factor.unsqueeze(2).broadcast_to([P, P // RUN, PACK, RUN])
-            nc.vector.tensor_tensor(to_columns(rounded[c][:, b * P : (b + 1) * P, :]), from_rows(rows), factor, MULT)
+            nc.vector.tensor_tensor(to_columns(rounded[c, b]), from_rows(rows), factor, MULT)
 
         def masked_bytes(c, b):
             return 4 * PACK * (c % 2 * CHUNK + b * P)
@@ -221,28 +227,35 @@ def tile_moe_bdx_glu_relu_kernel(
         def quantise(values, code, scale):
             nc.vector.quantize_mx(out=code.bitcast(E5M2X4), scales=scale, in_=values)
 
-        def hidden_gradient(c, pieces=1):
-            e = c * CHUNK // C
-            code = ring.tile([P, CHUNK], U32, name="g_code", align_bytes=64)
-            if c >= 2:
-                offset = masked_bytes(c, 1)
-                scale = two_places.tile([P, CHUNK], U8, name=f"g_scale_{c}", align_bytes=64, offset=offset)
+        g_code, g_scale = {}, {}
+
+        def quantise_g(c):
+            if c < 2:
+                g_code[c] = after_first.tile([P, CHUNK], U32, name=f"g_code_{c}", align_bytes=64, offset=2 * H * (c + 1))
+                g_scale[c] = ring.tile([P, CHUNK], U8, name="g_scale", align_bytes=64)
             else:
-                scale = ring.tile([P, CHUNK], U8, name="g_scale", align_bytes=64)
-            width = CHUNK // pieces
+                offset = masked_bytes(c, 1)
+                g_code[c] = ring.tile([P, CHUNK], U32, name="g_code", align_bytes=64)
+                g_scale[c] = two_places.tile([P, CHUNK], U8, name=f"g_scale_{c}", align_bytes=64, offset=offset)
+            if c > 0:
+                quantise(rounded[c].rearrange("p c t -> p (c t)"), g_code[c][:], g_scale[c][:])
+                return
             for b in range(BLOCKS):
                 block = slice(b * P, (b + 1) * P)
-                if b * P % width == 0:
-                    piece = slice(b * P, b * P + width)
-                    quantise(rounded[c][:, piece, :].rearrange("p c t -> p (c t)"), code[:, piece], scale[:, piece])
+                quantise(rounded[c, b].rearrange("p c t -> p (c t)"), g_code[c][:, block], g_scale[c][:, block])
+
+        def hidden_gradient(c):
+            e = c * CHUNK // C
+            for b in range(BLOCKS):
+                block = slice(b * P, (b + 1) * P)
                 bank = dh[c, b] = dh_banks.tile([P, PACK, P], F32, name="dh")
                 for t in range(PACK):
                     nc.tensor.matmul_mx(
                         out=bank[:, t, :],
                         lhsT=w2_code[e][:, 2 * P * t : 2 * P * (t + 1)].bitcast(E2M1X4),
                         lhsT_scale=w2_scale[:, e, P * t : P * (t + 1)],
-                        rhs=code[:, block].bitcast(E5M2X4),
-                        rhs_scale=scale[:, block],
+                        rhs=g_code[c][:, block].bitcast(E5M2X4),
+                        rhs_scale=g_scale[c][:, block],
                         start=True,
                         stop=True,
                     )
@@ -261,6 +274,9 @@ def tile_moe_bdx_glu_relu_kernel(
                 nc.vector.scalar_tensor_tensor(
                     masked[c, b], saved["a1", c][:, :, b * P : (b + 1) * P], 0.0, dh[c, b][:], IS_GT, MULT
                 )
+                if (c, b) == (0, 0):
+                    quantise_g(1)
+                    hidden_gradient(1)
 
         def first_product(engine, c, b):
             block = slice(b * P, (b + 1) * P)
@@ -294,10 +310,7 @@ def tile_moe_bdx_glu_relu_kernel(
         def input_gradient(c):
             e = c * CHUNK // C
             last = c == CHUNKS - 1
-            if c == 0:
-                code = after_first.tile([P, 2 * CHUNK], U32, name="da_code_0", align_bytes=64, offset=4 * H)
-            else:
-                code = ring.tile([P, 2 * CHUNK], U32, name="da_code", align_bytes=64)
+            code = ring.tile([P, 2 * CHUNK], U32, name="da_code", align_bytes=64)
             scale = ring.tile([P, 2 * CHUNK], U8, name="da_scale", align_bytes=64)
             quantise(da[c].rearrange("p a c t -> p (a c t)"), code[:], scale[:])
             dx = ring.tile([P, K_BLOCKS, CHUNK], F32, name="dx_out")
@@ -318,7 +331,8 @@ def tile_moe_bdx_glu_relu_kernel(
                     copy = nc.vector.tensor_copy if k else nc.scalar.copy
                     copy(dx[:, k, :], bank[:, k, :])
             if not last:
-                nc.scalar.copy(dx[:], bank[:])
+                for k in reversed(range(K_BLOCKS)):
+                    nc.scalar.copy(dx[:, k, :], bank[:, k, :])
             for k in reversed(range(K_BLOCKS)):
                 place = windows[k][:].indirect(entries(c * CHUNK, CHUNK))
                 if last and k:
@@ -326,18 +340,18 @@ def tile_moe_bdx_glu_relu_kernel(
                 else:
                     nc.scalar.activation(place, dx[:, k, :], COPY)
 
+        permute_w2_scale()
         for j in range(PACK - 1):
             gather_gated(j, 0, GATED)
             gather_ungated(j, GATED, CHUNKS)
-            if j == 1:
-                permute_w2(0)
-                permute_w2_scale()
-        for c in range(GATED):
+        permute_w2(0)
+        for c in range(GATED - 1):
             gather_gated(PACK - 1, c, c + 1)
-        round_gated(0, BLOCKS)
+        round_gated(0)
         round_gated(1)
-        hidden_gradient(0, BLOCKS)
-        hidden_gradient(1)
+        quantise_g(0)
+        hidden_gradient(0)
+        gather_gated(PACK - 1, GATED - 1, GATED)
         mask(0)
         gather_ungated(PACK - 1, GATED, GATED + 1)
         round_gated(2)
@@ -346,17 +360,21 @@ def tile_moe_bdx_glu_relu_kernel(
         round_gated(3)
         gather_ungated(PACK - 1, GATED + 2, GATED + 3)
         gather_ungated(PACK - 1, GATED + 3, CHUNKS)
+        permute_w2(2)
+        permute_w2(3)
         blocks = list(range(GATED * BLOCKS, CHUNKS * BLOCKS))
         for c in range(CHUNKS):
             products(c)
-            for block in blocks[: (1, 1, 2, 2, 1, 1, 0, 0)[c]]:
+            for block in blocks[: (1, 1, 1, 2, 2, 1, 0, 0)[c]]:
                 gate_and_round(blocks.pop(0))
             if c + 1 < CHUNKS:
                 mask(c + 1)
-            if c + 2 < CHUNKS:
+            if 0 < c < CHUNKS - 2:
+                quantise_g(c + 2)
                 hidden_gradient(c + 2)
             input_gradient(c)
-            if c < 2:
-                permute_w2(c + 2)
+            if c == 0:
+                quantise_g(c + 2)
+                hidden_gradient(c + 2)
         for k, queue in enumerate((nc.scalar, nc.sync)):
             queue.dma_start(out[k * P : (k + 1) * P, :], windows[k][:])

@@ -15,6 +15,8 @@ BLOCKS = CHUNK // P
 RUN = 4
 GATED = CHUNKS // 2
 
+JOINT_AT = (6, 10, 14, 0, 4, 12, 2)
+
 FLOPS = 2 * E * C * (N * H + 2 * H * K)
 WEIGHTS = E * (N * H + 2 * H * K)
 BYTES = 4 * (N * T + 2 * H * E * C + E * C + K * T) + WEIGHTS // 2 + WEIGHTS // 32 + 2 * P * (E * C // LIST_ROWS)
@@ -40,7 +42,6 @@ def tile_moe_bdx_glu_relu_kernel(
     with ExitStack() as ctx:
         held = ctx.enter_context(tc.tile_pool(name="held", bufs=1))
         ring = ctx.enter_context(tc.tile_pool(name="ring", bufs=3))
-        joints = ctx.enter_context(tc.tile_pool(name="joints", bufs=1))
         after_gates = ctx.enter_context(tc.tile_pool(name="after_gates", bufs=1))
         after_first = ctx.enter_context(tc.tile_pool(name="after_first", bufs=1))
         after_plane = ctx.enter_context(tc.tile_pool(name="after_plane", bufs=1))
@@ -113,23 +114,27 @@ def tile_moe_bdx_glu_relu_kernel(
         load_plane(2)
         load_plane(3)
         load_saved("a1", a1, 0, CHUNK)
-        load_saved("a3", a3, 0, CHUNK)
         load_saved("a1", a1, CHUNK, CHUNK)
+        load_saved("a3", a3, 0, CHUNK)
+        slot_gates = held.tile([P, BLOCKS], F32, name="slot_gates")
+        with nc.allow_non_contiguous_dma(reason="one gate a partition for each block of slots"):
+            nc.sync.dma_start(slot_gates[:], gate[0, 2 * C : 2 * C + CHUNK].rearrange("(b p) -> p b", p=P))
         load_w2(1)
         load_scales(w1_scale, w1_scales)
         w1_code = load_words("w1_code", w1_words, 0, E)
         w3_code = load_words("w3_code", w3_words, 0, E)
         load_scales(w3_scale, w3_scales)
+        load_saved("a1", a1, 2 * CHUNK, CHUNK)
         load_saved("a3", a3, CHUNK, CHUNK)
         load_w2(2)
         load_w2(3)
-        load_saved("a1", a1, 2 * CHUNK, CHUNK)
-        load_saved("a3", a3, 2 * CHUNK, CHUNK)
         load_saved("a1", a1, 3 * CHUNK, CHUNK)
+        load_saved("a3", a3, 2 * CHUNK, CHUNK)
+        load_saved("a1", a1, 2 * C, C)
         load_saved("a3", a3, 3 * CHUNK, CHUNK)
-        for e in (2, 3):
-            load_saved("a1", a1, e * C, C)
-            load_saved("a3", a3, e * C, C)
+        load_saved("a1", a1, 3 * C, C)
+        load_saved("a3", a3, 2 * C, C)
+        load_saved("a3", a3, 3 * C, C)
 
         def spread_gates(e, pool, name):
             bank = pool.tile([P, PACK, P], F32, name=name)
@@ -187,21 +192,22 @@ def tile_moe_bdx_glu_relu_kernel(
             nc.scalar.activation(place, planes[j][:].indirect(entries(first * CHUNK, (last - first) * CHUNK)), COPY)
 
         rounded, dh, da, masked = {}, {}, {}, {}
+        joint = held.tile([P, (max(JOINT_AT) + 6) * P * PACK], BF16, name="joint", align_bytes=64)
 
         def place_rounded(c):
             if c == 0:
                 rounded[c, 0] = flat[:, -CHUNK:].bitcast(BF16).rearrange("p (c t) -> p c t", t=PACK)
                 rounded[c, 1] = after_first.tile([P, P, PACK], BF16, name="rounded_0", align_bytes=64, offset=6 * H)[:]
                 return
-            offset = (c - 1 if c <= GATED else c - GATED) * 4 * CHUNK * PACK
-            halves = 3 if c == CHUNKS - 1 else 2
-            tile = joints.tile([P, halves, CHUNK, PACK], BF16, name=f"joint_{c}", align_bytes=64, offset=offset)
+            first = JOINT_AT[c - 1] * P * PACK
+            both = joint[:, first : first + 3 * CHUNK * PACK].rearrange("p (a c t) -> p a c t", a=3, t=PACK)
             if c == CHUNKS - 1:
-                da[c] = tile[:, 1:3]
-            da[c - 1] = tile[:, 0:2]
-            rounded[c] = tile[:, 0]
+                da[c] = both[:, 1:3]
+            da[c - 1] = both[:, 0:2]
+            middle = joint[:, first + P * PACK : first + 3 * P * PACK]
+            rounded[c] = middle.rearrange("p (c t) -> p c t", t=PACK)
             for b in range(BLOCKS):
-                rounded[c, b] = tile[:, 0, b * P : (b + 1) * P, :]
+                rounded[c, b] = rounded[c][:, b * P : (b + 1) * P, :]
 
         def round_gated(c):
             place_rounded(c)
@@ -220,6 +226,28 @@ def tile_moe_bdx_glu_relu_kernel(
             factor = gates_in_psum[e][:, first // RUN : (first + P) // RUN, :]
             factor = factor.unsqueeze(2).broadcast_to([P, P // RUN, PACK, RUN])
             nc.vector.tensor_tensor(to_columns(rounded[c, b]), from_rows(rows), factor, MULT)
+
+        turned = {}
+
+        def gate_turned(block):
+            rows = ungated[:, :, block * P - GATED * CHUNK : (block + 1) * P - GATED * CHUNK]
+            bank = dx_banks.tile([P, PACK, P], F32, name="dx")
+            for t in range(PACK):
+                nc.tensor.transpose(bank[:, t, :], rows[:, t, :], identity[:])
+            turned[block] = ring.tile([P, 2, P, 2], BF16, name="turned", align_bytes=64)
+            factor = slot_gates[:, block % PACK : block % PACK + 1]
+            nc.scalar.activation(turned[block][:], bank[:].rearrange("s (u e) p -> s u p e", e=2), COPY, scale=factor)
+
+        def turn_back(block):
+            c, b = divmod(block, BLOCKS)
+            if b == 0:
+                place_rounded(c)
+            words = turned[block][:].rearrange("s u p e -> s (u p e)").bitcast(F32)
+            bank = dx_banks.tile([P, 2, P], F32, name="dx")
+            for u in range(2):
+                nc.tensor.transpose(bank[:, u, :], words[:, u * P : (u + 1) * P], identity[:])
+            place = rounded[c, b].rearrange("p s t -> p (s t)").bitcast(F32).rearrange("p (s u) -> p s u", u=2)
+            nc.scalar.copy(place, bank[:].rearrange("p u s -> p s u"))
 
         def masked_bytes(c, b):
             return 4 * PACK * (c % 2 * CHUNK + b * P)
@@ -353,19 +381,22 @@ def tile_moe_bdx_glu_relu_kernel(
         hidden_gradient(0)
         gather_gated(PACK - 1, GATED - 1, GATED)
         mask(0)
-        gather_ungated(PACK - 1, GATED, GATED + 1)
+        gather_ungated(PACK - 1, GATED, GATED + 2)
         round_gated(2)
+        gate_turned(8)
         permute_w2(1)
-        gather_ungated(PACK - 1, GATED + 1, GATED + 2)
+        turn_back(8)
+        gate_turned(9)
         round_gated(3)
+        turn_back(9)
         gather_ungated(PACK - 1, GATED + 2, GATED + 3)
         gather_ungated(PACK - 1, GATED + 3, CHUNKS)
         permute_w2(2)
         permute_w2(3)
-        blocks = list(range(GATED * BLOCKS, CHUNKS * BLOCKS))
+        blocks = list(range((GATED + 1) * BLOCKS, CHUNKS * BLOCKS))
         for c in range(CHUNKS):
             products(c)
-            for block in blocks[: (1, 1, 1, 2, 2, 1, 0, 0)[c]]:
+            for block in blocks[: (1, 1, 1, 1, 1, 1, 0, 0)[c]]:
                 gate_and_round(blocks.pop(0))
             if c + 1 < CHUNKS:
                 mask(c + 1)

@@ -10,12 +10,13 @@ PACK = 4
 K_BLOCKS = K // P
 LIST_ROWS = 16
 CHUNK = 256
+BANK = 2048
 CHUNKS = E * C // CHUNK
 BLOCKS = CHUNK // P
 RUN = 4
 GATED = CHUNKS // 2
 
-JOINT_AT = (6, 10, 14, 0, 4, 12, 2)
+JOINT_AT = (6, 10, 0, 4, 8, 2, 6)
 
 FLOPS = 2 * E * C * (N * H + 2 * H * K)
 WEIGHTS = E * (N * H + 2 * H * K)
@@ -46,7 +47,7 @@ def tile_moe_bdx_glu_relu_kernel(
         after_first = ctx.enter_context(tc.tile_pool(name="after_first", bufs=1))
         after_plane = ctx.enter_context(tc.tile_pool(name="after_plane", bufs=1))
         two_places = ctx.enter_context(tc.tile_pool(name="two_places", bufs=1))
-        dh_banks = ctx.enter_context(tc.psum_pool(name="dh_banks", bufs=2 * BLOCKS))
+        dh_banks = ctx.enter_context(tc.psum_pool(name="dh_banks", bufs=1))
         dx_banks = ctx.enter_context(tc.psum_pool(name="dx_banks", bufs=2))
         gate_banks = ctx.enter_context(tc.psum_pool(name="gate_banks", bufs=2))
 
@@ -113,27 +114,31 @@ def tile_moe_bdx_glu_relu_kernel(
         gate_columns[2], gate_columns[3] = late[:, 0], late[:, 1]
         load_plane(2)
         load_plane(3)
+        w_code = {}
+
+        def load_w13(first):
+            for name, dram in (("w1", w1_words), ("w3", w3_words)):
+                tile = load_words(f"{name}_code_{first}", dram, first, first + 2)
+                w_code[name, first], w_code[name, first + 1] = tile[:, 0], tile[:, 1]
+
         load_saved("a1", a1, 0, CHUNK)
-        load_saved("a1", a1, CHUNK, CHUNK)
         load_saved("a3", a3, 0, CHUNK)
-        slot_gates = held.tile([P, BLOCKS], F32, name="slot_gates")
-        with nc.allow_non_contiguous_dma(reason="one gate a partition for each block of slots"):
-            nc.sync.dma_start(slot_gates[:], gate[0, 2 * C : 2 * C + CHUNK].rearrange("(b p) -> p b", p=P))
-        load_w2(1)
+        load_saved("a1", a1, CHUNK, CHUNK)
+        others = load_words("w2_raw_1", w2_words, 1, E)
+        for e in range(1, E):
+            w2_raw[e] = others[:, e - 1]
         load_scales(w1_scale, w1_scales)
-        w1_code = load_words("w1_code", w1_words, 0, E)
-        w3_code = load_words("w3_code", w3_words, 0, E)
+        load_w13(0)
         load_scales(w3_scale, w3_scales)
         load_saved("a1", a1, 2 * CHUNK, CHUNK)
         load_saved("a3", a3, CHUNK, CHUNK)
-        load_w2(2)
-        load_w2(3)
-        load_saved("a1", a1, 3 * CHUNK, CHUNK)
         load_saved("a3", a3, 2 * CHUNK, CHUNK)
-        load_saved("a1", a1, 2 * C, C)
+        load_saved("a1", a1, 3 * CHUNK, CHUNK)
         load_saved("a3", a3, 3 * CHUNK, CHUNK)
-        load_saved("a1", a1, 3 * C, C)
+        load_saved("a1", a1, 2 * C, C)
+        load_w13(2)
         load_saved("a3", a3, 2 * C, C)
+        load_saved("a1", a1, 3 * C, C)
         load_saved("a3", a3, 3 * C, C)
 
         def spread_gates(e, pool, name):
@@ -227,28 +232,6 @@ def tile_moe_bdx_glu_relu_kernel(
             factor = factor.unsqueeze(2).broadcast_to([P, P // RUN, PACK, RUN])
             nc.vector.tensor_tensor(to_columns(rounded[c, b]), from_rows(rows), factor, MULT)
 
-        turned = {}
-
-        def gate_turned(block):
-            rows = ungated[:, :, block * P - GATED * CHUNK : (block + 1) * P - GATED * CHUNK]
-            bank = dx_banks.tile([P, PACK, P], F32, name="dx")
-            for t in range(PACK):
-                nc.tensor.transpose(bank[:, t, :], rows[:, t, :], identity[:])
-            turned[block] = ring.tile([P, 2, P, 2], BF16, name="turned", align_bytes=64)
-            factor = slot_gates[:, block % PACK : block % PACK + 1]
-            nc.scalar.activation(turned[block][:], bank[:].rearrange("s (u e) p -> s u p e", e=2), COPY, scale=factor)
-
-        def turn_back(block):
-            c, b = divmod(block, BLOCKS)
-            if b == 0:
-                place_rounded(c)
-            words = turned[block][:].rearrange("s u p e -> s (u p e)").bitcast(F32)
-            bank = dx_banks.tile([P, 2, P], F32, name="dx")
-            for u in range(2):
-                nc.tensor.transpose(bank[:, u, :], words[:, u * P : (u + 1) * P], identity[:])
-            place = rounded[c, b].rearrange("p s t -> p (s t)").bitcast(F32).rearrange("p (s u) -> p s u", u=2)
-            nc.scalar.copy(place, bank[:].rearrange("p u s -> p s u"))
-
         def masked_bytes(c, b):
             return 4 * PACK * (c % 2 * CHUNK + b * P)
 
@@ -276,7 +259,8 @@ def tile_moe_bdx_glu_relu_kernel(
             e = c * CHUNK // C
             for b in range(BLOCKS):
                 block = slice(b * P, (b + 1) * P)
-                bank = dh[c, b] = dh_banks.tile([P, PACK, P], F32, name="dh")
+                offset = (c % 2 * BLOCKS + b) * BANK
+                bank = dh[c, b] = dh_banks.tile([P, PACK, P], F32, name=f"dh_{c}_{b}", offset=offset)
                 for t in range(PACK):
                     nc.tensor.matmul_mx(
                         out=bank[:, t, :],
@@ -343,22 +327,24 @@ def tile_moe_bdx_glu_relu_kernel(
             quantise(da[c].rearrange("p a c t -> p (a c t)"), code[:], scale[:])
             dx = ring.tile([P, K_BLOCKS, CHUNK], F32, name="dx_out")
             for k in reversed(range(K_BLOCKS)):
-                if k == K_BLOCKS - 1 or last:
+                if c == 0:
+                    bank = dh_banks.tile([P, K_BLOCKS, CHUNK], F32, name=f"dx_0_{k}", offset=(1 - k) * BANK)
+                elif k == K_BLOCKS - 1 or last:
                     bank = dx_banks.tile([P, K_BLOCKS, CHUNK], F32, name="dx")
-                for a, (w_code, w_scale) in enumerate(((w1_code, w1_scale), (w3_code, w3_scale))):
+                for a, (name, w_scale) in enumerate((("w1", w1_scale), ("w3", w3_scale))):
                     nc.tensor.matmul_mx(
                         out=bank[:, k, :],
-                        lhsT=w_code[:, e, 2 * P * k : 2 * P * (k + 1)].bitcast(E2M1X4),
+                        lhsT=w_code[name, e][:, 2 * P * k : 2 * P * (k + 1)].bitcast(E2M1X4),
                         lhsT_scale=w_scale[:, e, P * k : P * (k + 1)],
                         rhs=code[:, a * CHUNK : (a + 1) * CHUNK].bitcast(E5M2X4),
                         rhs_scale=scale[:, a * CHUNK : (a + 1) * CHUNK],
                         start=a == 0,
                         stop=a == 1,
                     )
-                if last:
-                    copy = nc.vector.tensor_copy if k else nc.scalar.copy
+                if c in (0, CHUNKS - 1):
+                    copy = nc.vector.tensor_copy if k and last else nc.scalar.copy
                     copy(dx[:, k, :], bank[:, k, :])
-            if not last:
+            if 0 < c < CHUNKS - 1:
                 for k in reversed(range(K_BLOCKS)):
                     nc.scalar.copy(dx[:, k, :], bank[:, k, :])
             for k in reversed(range(K_BLOCKS)):
@@ -383,20 +369,16 @@ def tile_moe_bdx_glu_relu_kernel(
         mask(0)
         gather_ungated(PACK - 1, GATED, GATED + 2)
         round_gated(2)
-        gate_turned(8)
         permute_w2(1)
-        turn_back(8)
-        gate_turned(9)
         round_gated(3)
-        turn_back(9)
         gather_ungated(PACK - 1, GATED + 2, GATED + 3)
         gather_ungated(PACK - 1, GATED + 3, CHUNKS)
         permute_w2(2)
         permute_w2(3)
-        blocks = list(range((GATED + 1) * BLOCKS, CHUNKS * BLOCKS))
+        blocks = list(range(GATED * BLOCKS, CHUNKS * BLOCKS))
         for c in range(CHUNKS):
             products(c)
-            for block in blocks[: (1, 1, 1, 1, 1, 1, 0, 0)[c]]:
+            for block in blocks[: (1, 2, 1, 1, 2, 1, 0, 0)[c]]:
                 gate_and_round(blocks.pop(0))
             if c + 1 < CHUNKS:
                 mask(c + 1)

@@ -46,6 +46,7 @@ def tile_moe_bdx_glu_relu_kernel(
         after_gates = ctx.enter_context(tc.tile_pool(name="after_gates", bufs=1))
         after_first = ctx.enter_context(tc.tile_pool(name="after_first", bufs=1))
         after_plane = ctx.enter_context(tc.tile_pool(name="after_plane", bufs=1))
+        after_a1 = ctx.enter_context(tc.tile_pool(name="after_a1", bufs=1))
         two_places = ctx.enter_context(tc.tile_pool(name="two_places", bufs=1))
         dh_banks = ctx.enter_context(tc.psum_pool(name="dh_banks", bufs=1))
         dx_banks = ctx.enter_context(tc.psum_pool(name="dx_banks", bufs=2))
@@ -95,7 +96,10 @@ def tile_moe_bdx_glu_relu_kernel(
         saved = {}
 
         def load_saved(name, dram, first, count):
-            tile = held.tile([P, PACK, count], F32, name=f"{name}_{first}", align_bytes=64)
+            if (name, first) == ("a1", 3 * C):
+                tile = after_a1.tile([P, PACK, count], F32, name="a1_last", align_bytes=64, offset=0)
+            else:
+                tile = held.tile([P, PACK, count], F32, name=f"{name}_{first}", align_bytes=64)
             nc.sync.dma_start(tile[:], dram.rearrange("(p t) s -> p t s", t=PACK)[:, :, first : first + count])
             for c in range(count // CHUNK):
                 saved[name, first // CHUNK + c] = tile[:, :, c * CHUNK : (c + 1) * CHUNK]
@@ -209,7 +213,8 @@ def tile_moe_bdx_glu_relu_kernel(
             if c == CHUNKS - 1:
                 da[c] = both[:, 1:3]
             da[c - 1] = both[:, 0:2]
-            middle = joint[:, first + P * PACK : first + 3 * P * PACK]
+            start = first if c == 1 else first + P * PACK
+            middle = joint[:, start : start + CHUNK * PACK]
             rounded[c] = middle.rearrange("p (c t) -> p c t", t=PACK)
             for b in range(BLOCKS):
                 rounded[c, b] = rounded[c][:, b * P : (b + 1) * P, :]
@@ -316,21 +321,41 @@ def tile_moe_bdx_glu_relu_kernel(
                 )
             if c == CHUNKS - 1:
                 first_product(nc.vector, c, 1)
+                copy_dx(c - 1, 1)
 
         windows = [held.tile([P, T], F32, name=f"window_{k}") for k in range(K_BLOCKS)]
 
+        dx, dx_bank = {}, {}
+
+        def on_vector(c, k):
+            return k == 1 and c >= CHUNKS - 2
+
+        def copy_dx(c, k):
+            copy = nc.vector.tensor_copy if on_vector(c, k) else nc.scalar.copy
+            copy(dx[c][:, k, :], dx_bank[c, k][:, k, :])
+
+        def scatter(c, k):
+            place = windows[k][:].indirect(entries(c * CHUNK, CHUNK))
+            if on_vector(c, k):
+                nc.vector.tensor_copy(place, dx[c][:, k, :])
+            else:
+                nc.scalar.activation(place, dx[c][:, k, :], COPY)
+
         def input_gradient(c):
             e = c * CHUNK // C
-            last = c == CHUNKS - 1
             code = ring.tile([P, 2 * CHUNK], U32, name="da_code", align_bytes=64)
             scale = ring.tile([P, 2 * CHUNK], U8, name="da_scale", align_bytes=64)
             quantise(da[c].rearrange("p a c t -> p (a c t)"), code[:], scale[:])
-            dx = ring.tile([P, K_BLOCKS, CHUNK], F32, name="dx_out")
+            if c == CHUNKS - 2:
+                dx[c] = after_a1.tile([P, K_BLOCKS, CHUNK], F32, name="dx_late", align_bytes=64, offset=0)
+            else:
+                dx[c] = ring.tile([P, K_BLOCKS, CHUNK], F32, name="dx_out")
             for k in reversed(range(K_BLOCKS)):
-                if c == 0:
-                    bank = dh_banks.tile([P, K_BLOCKS, CHUNK], F32, name=f"dx_0_{k}", offset=(1 - k) * BANK)
-                elif k == K_BLOCKS - 1 or last:
+                if c in (0, CHUNKS - 1):
+                    bank = dh_banks.tile([P, K_BLOCKS, CHUNK], F32, name=f"dx_{c}_{k}", offset=(1 - k) * BANK)
+                elif k == K_BLOCKS - 1:
                     bank = dx_banks.tile([P, K_BLOCKS, CHUNK], F32, name="dx")
+                dx_bank[c, k] = bank
                 for a, (name, w_scale) in enumerate((("w1", w1_scale), ("w3", w3_scale))):
                     nc.tensor.matmul_mx(
                         out=bank[:, k, :],
@@ -341,18 +366,12 @@ def tile_moe_bdx_glu_relu_kernel(
                         start=a == 0,
                         stop=a == 1,
                     )
-                if c in (0, CHUNKS - 1):
-                    copy = nc.vector.tensor_copy if k and last else nc.scalar.copy
-                    copy(dx[:, k, :], bank[:, k, :])
-            if 0 < c < CHUNKS - 1:
-                for k in reversed(range(K_BLOCKS)):
-                    nc.scalar.copy(dx[:, k, :], bank[:, k, :])
-            for k in reversed(range(K_BLOCKS)):
-                place = windows[k][:].indirect(entries(c * CHUNK, CHUNK))
-                if last and k:
-                    nc.vector.tensor_copy(place, dx[:, k, :])
-                else:
-                    nc.scalar.activation(place, dx[:, k, :], COPY)
+
+        def bring_back(c, halves):
+            for k in halves:
+                copy_dx(c, k)
+            for k in halves:
+                scatter(c, k)
 
         permute_w2_scale()
         for j in range(PACK - 1):
@@ -386,6 +405,11 @@ def tile_moe_bdx_glu_relu_kernel(
                 quantise_g(c + 2)
                 hidden_gradient(c + 2)
             input_gradient(c)
+            if c == CHUNKS - 1:
+                scatter(c - 1, 1)
+                bring_back(c - 1, (0,))
+            if c != CHUNKS - 2:
+                bring_back(c, (1, 0))
             if c == 0:
                 quantise_g(c + 2)
                 hidden_gradient(c + 2)

from contextlib import ExitStack

import concourse.mybir as mybir
from concourse.masks import make_identity

K, T, E, C, H, N = 256, 2048, 4, 512, 512, 512

P = 128
PACK = 4
K_BLOCKS = K // P
LIST_ROWS = 16
CHUNK = 256
BANK = 2048
CHUNKS = E * C // CHUNK
BLOCKS = CHUNK // P
RUN = 4
GATED = CHUNKS // 2

JOINT_AT = (6, 10, 0, 4, 8, 2, 6)

FLOPS = 2 * E * C * (N * H + 2 * H * K)
WEIGHTS = E * (N * H + 2 * H * K)
BYTES = 4 * (N * T + 2 * H * E * C + E * C + K * T) + WEIGHTS // 2 + WEIGHTS // 32 + 2 * P * (E * C // LIST_ROWS)

F32 = mybir.dt.float32
BF16 = mybir.dt.bfloat16
I32 = mybir.dt.int32
U32 = mybir.dt.uint32
U16 = mybir.dt.uint16
U8 = mybir.dt.uint8
E5M2X4 = mybir.dt.float8_e5m2_x4
E2M1X4 = mybir.dt.float4_e2m1fn_x4
MULT = mybir.AluOpType.mult
MAX = mybir.AluOpType.max
IS_GT = mybir.AluOpType.is_gt
COPY = mybir.ActivationFunctionType.Copy


def tile_moe_bdx_glu_relu_kernel(
    tc, dyT, a1, a3, w2_words, w2_scales, w1_words, w1_scales, w3_words, w3_scales, gate, offs, out
):
    nc = tc.nc
    with ExitStack() as ctx:
        held = ctx.enter_context(tc.tile_pool(name="held", bufs=1))
        ring = ctx.enter_context(tc.tile_pool(name="ring", bufs=3))
        after_gates = ctx.enter_context(tc.tile_pool(name="after_gates", bufs=1))
        after_first = ctx.enter_context(tc.tile_pool(name="after_first", bufs=1))
        after_plane = ctx.enter_context(tc.tile_pool(name="after_plane", bufs=1))
        after_a1 = ctx.enter_context(tc.tile_pool(name="after_a1", bufs=1))
        two_places = ctx.enter_context(tc.tile_pool(name="two_places", bufs=1))
        dh_banks = ctx.enter_context(tc.psum_pool(name="dh_banks", bufs=1))
        dx_banks = ctx.enter_context(tc.psum_pool(name="dx_banks", bufs=2))
        gate_banks = ctx.enter_context(tc.psum_pool(name="gate_banks", bufs=2))

        offsets = held.tile([P, E * C // LIST_ROWS], U16, name="offsets")

        def entries(first, count):
            return offsets[:, first // LIST_ROWS : (first + count) // LIST_ROWS]

        def load_words(name, dram, first, last):
            tile = held.tile([P, last - first, dram.shape[3]], U8, name=name, align_bytes=64)
            nc.sync.dma_start(tile[:].bitcast(I32), dram[first:last].rearrange("e s p b -> p (e s) b").bitcast(I32))
            return tile

        def load_scales(tile, dram):
            for q in range(4):
                nc.sync.dma_start(
                    tile[32 * q : 32 * q + 4].bitcast(I32),
                    dram[:, 0, 4 * q : 4 * q + 4, :].rearrange("e f i -> f e i").bitcast(I32),
                )

        w2_scale_raw = held.tile([P, E, H], U8, name="w2_scale_raw", align_bytes=64)
        w1_scale = held.tile([P, E, K], U8, name="w1_scale", align_bytes=64)
        w3_scale = held.tile([P, E, K], U8, name="w3_scale", align_bytes=64)
        nc.vector.memset(w2_scale_raw[:].bitcast(I32), 0)
        identity = held.tile([P, P], F32, name="identity")
        make_identity(nc, identity[:])
        for tile in (w1_scale, w3_scale):
            nc.gpsimd.memset(tile[:].bitcast(I32), 0)

        early = after_gates.tile([P, 2, 2 * PACK], F32, name="gate_columns", align_bytes=64, offset=0)
        nc.sync.dma_start(early[:, :, 0:PACK], gate[0, : 2 * C].rearrange("(e p c) -> p e c", e=2, c=PACK))
        gate_columns = {0: early[:, 0], 1: early[:, 1]}
        nc.sync.dma_start(offsets[:], offs)
        load_scales(w2_scale_raw, w2_scales)

        planes = {}

        def load_plane(j):
            if j == 2:
                planes[j] = after_plane.tile([P, T], F32, name="plane_2", align_bytes=64, offset=0)
            else:
                planes[j] = held.tile([P, T], F32, name=f"plane_{j}")
            nc.sync.dma_start(planes[j][:], dyT.rearrange("(p j) s -> p j s", j=PACK)[:, j, :])

        saved = {}

        def load_saved(name, dram, first, count):
            if (name, first) == ("a1", 3 * C):
                tile = after_a1.tile([P, PACK, count], F32, name="a1_last", align_bytes=64, offset=0)
            else:
                tile = held.tile([P, PACK, count], F32, name=f"{name}_{first}", align_bytes=64)
            nc.sync.dma_start(tile[:], dram.rearrange("(p t) s -> p t s", t=PACK)[:, :, first : first + count])
            for c in range(count // CHUNK):
                saved[name, first // CHUNK + c] = tile[:, :, c * CHUNK : (c + 1) * CHUNK]

        w2_raw = {}

        def load_w2(e):
            w2_raw[e] = held.tile([P, 2 * H], U8, name=f"w2_raw_{e}", align_bytes=64)
            nc.sync.dma_start(w2_raw[e][:].bitcast(I32), w2_words[e, 0].bitcast(I32))

        load_plane(0)
        load_plane(1)
        load_w2(0)
        late = held.tile([P, 2, 2 * PACK], F32, name="gate_columns_late")
        nc.sync.dma_start(late[:, :, 0:PACK], gate[0, 2 * C :].rearrange("(e p c) -> p e c", e=2, c=PACK))
        gate_columns[2], gate_columns[3] = late[:, 0], late[:, 1]
        load_plane(2)
        load_plane(3)
        w_code = {}

        def load_w13(first):
            for name, dram in (("w1", w1_words), ("w3", w3_words)):
                tile = load_words(f"{name}_code_{first}", dram, first, first + 2)
                w_code[name, first], w_code[name, first + 1] = tile[:, 0], tile[:, 1]

        load_saved("a1", a1, 0, CHUNK)
        load_saved("a3", a3, 0, CHUNK)
        load_saved("a1", a1, CHUNK, CHUNK)
        others = load_words("w2_raw_1", w2_words, 1, E)
        for e in range(1, E):
            w2_raw[e] = others[:, e - 1]
        load_scales(w1_scale, w1_scales)
        load_w13(0)
        load_scales(w3_scale, w3_scales)
        load_saved("a1", a1, 2 * CHUNK, CHUNK)
        load_saved("a3", a3, CHUNK, CHUNK)
        load_saved("a3", a3, 2 * CHUNK, CHUNK)
        load_saved("a1", a1, 3 * CHUNK, CHUNK)
        load_saved("a3", a3, 3 * CHUNK, CHUNK)
        load_saved("a1", a1, 2 * C, C)
        load_w13(2)
        load_saved("a3", a3, 2 * C, C)
        load_saved("a1", a1, 3 * C, C)
        load_saved("a3", a3, 3 * C, C)

        def spread_gates(e, pool, name):
            bank = pool.tile([P, PACK, P], F32, name=name)
            for c in range(PACK):
                nc.tensor.transpose(bank[:, c, :], gate_columns[e][:, c : c + 1].to_broadcast([P, P]), identity[:])
            return bank[:].rearrange("p c n -> p n c")

        gates = held.tile([P, 2 * C], F32, name="gates")
        for e in range(2):
            place = gates[:, e * C : (e + 1) * C].rearrange("p (n c) -> p n c", c=PACK)
            if e == 0:
                nc.vector.tensor_copy(place, spread_gates(e, dx_banks, "dx"))
            else:
                nc.scalar.activation(place, spread_gates(e, dx_banks, "dx"), COPY)
        gates_in_psum = {e: spread_gates(e, gate_banks, "gate_bank") for e in range(2, E)}

        w2_scale = held.tile([P, E, H], U8, name="w2_scale", align_bytes=64)
        w2_code = {}

        def permute_w2_scale():
            nc.vector.tensor_copy(
                w2_scale[:].rearrange("p e (t m) -> p e t m", t=PACK),
                w2_scale_raw[:].rearrange("p e (m t) -> p e t m", t=PACK),
            )

        def permute_w2(e):
            if e == 0:
                w2_code[e] = after_plane.tile([P, 2 * H], U8, name="w2_code_0", align_bytes=64, offset=0)
            else:
                w2_code[e] = after_first.tile([P, 2 * H], U8, name=f"w2_code_{e}", align_bytes=64, offset=2 * H * e)
            nc.scalar.copy(
                w2_code[e][:].bitcast(U16).rearrange("p (t m) -> p t m", t=PACK),
                w2_raw[e][:].bitcast(U16).rearrange("p (m t) -> p t m", t=PACK),
            )

        def from_rows(ap):
            return ap.rearrange("p t (n c) -> p n t c", c=RUN)

        def to_columns(ap):
            return ap.rearrange("p (n c) t -> p n t c", c=RUN)

        row = GATED * CHUNK
        flat = after_gates.tile([P, (2 * PACK - 1) * row], F32, name="gathered", align_bytes=64, offset=0)
        gathered = flat[:].rearrange("p (r s) -> p r s", s=row)
        gated = gathered[:, PACK - 1 :, :]
        ungated = gathered[:, :PACK, :]

        def gather_gated(j, first, last):
            columns = slice(first * CHUNK, last * CHUNK)
            chosen = entries(columns.start, columns.stop - columns.start)
            nc.vector.tensor_tensor(gated[:, j, columns], planes[j][:].indirect(chosen), gates[:, columns], MULT)

        def gather_ungated(j, first, last):
            place = ungated[:, j, (first - GATED) * CHUNK : (last - GATED) * CHUNK]
            nc.scalar.activation(place, planes[j][:].indirect(entries(first * CHUNK, (last - first) * CHUNK)), COPY)

        rounded, dh, da, masked = {}, {}, {}, {}
        joint = held.tile([P, (max(JOINT_AT) + 6) * P * PACK], BF16, name="joint", align_bytes=64)

        def place_rounded(c):
            if c == 0:
                rounded[c, 0] = flat[:, -CHUNK:].bitcast(BF16).rearrange("p (c t) -> p c t", t=PACK)
                rounded[c, 1] = after_first.tile([P, P, PACK], BF16, name="rounded_0", align_bytes=64, offset=6 * H)[:]
                return
            first = JOINT_AT[c - 1] * P * PACK
            both = joint[:, first : first + 3 * CHUNK * PACK].rearrange("p (a c t) -> p a c t", a=3, t=PACK)
            if c == CHUNKS - 1:
                da[c] = both[:, 1:3]
            da[c - 1] = both[:, 0:2]
            start = first if c == 1 else first + P * PACK
            middle = joint[:, start : start + CHUNK * PACK]
            rounded[c] = middle.rearrange("p (c t) -> p c t", t=PACK)
            for b in range(BLOCKS):
                rounded[c, b] = rounded[c][:, b * P : (b + 1) * P, :]

        def round_gated(c):
            place_rounded(c)
            if c > 0:
                nc.scalar.activation(to_columns(rounded[c]), from_rows(gated[:, :, c * CHUNK : (c + 1) * CHUNK]), COPY)
                return
            for b in range(BLOCKS):
                nc.scalar.activation(to_columns(rounded[c, b]), from_rows(gated[:, :, b * P : (b + 1) * P]), COPY)

        def gate_and_round(block):
            c, b = divmod(block, BLOCKS)
            if b == 0:
                place_rounded(c)
            e, first = divmod(block * P, C)
            rows = ungated[:, :, block * P - GATED * CHUNK : (block + 1) * P - GATED * CHUNK]
            factor = gates_in_psum[e][:, first // RUN : (first + P) // RUN, :]
            factor = factor.unsqueeze(2).broadcast_to([P, P // RUN, PACK, RUN])
            nc.vector.tensor_tensor(to_columns(rounded[c, b]), from_rows(rows), factor, MULT)

        def masked_bytes(c, b):
            return 4 * PACK * (c % 2 * CHUNK + b * P)

        def quantise(values, code, scale):
            nc.vector.quantize_mx(out=code.bitcast(E5M2X4), scales=scale, in_=values)

        g_code, g_scale = {}, {}

        def quantise_g(c):
            if c < 2:
                g_code[c] = after_first.tile([P, CHUNK], U32, name=f"g_code_{c}", align_bytes=64, offset=2 * H * (c + 1))
                g_scale[c] = ring.tile([P, CHUNK], U8, name="g_scale", align_bytes=64)
            else:
                offset = masked_bytes(c, 1)
                g_code[c] = ring.tile([P, CHUNK], U32, name="g_code", align_bytes=64)
                g_scale[c] = two_places.tile([P, CHUNK], U8, name=f"g_scale_{c}", align_bytes=64, offset=offset)
            if c > 0:
                quantise(rounded[c].rearrange("p c t -> p (c t)"), g_code[c][:], g_scale[c][:])
                return
            for b in range(BLOCKS):
                block = slice(b * P, (b + 1) * P)
                quantise(rounded[c, b].rearrange("p c t -> p (c t)"), g_code[c][:, block], g_scale[c][:, block])

        def hidden_gradient(c):
            e = c * CHUNK // C
            for b in range(BLOCKS):
                block = slice(b * P, (b + 1) * P)
                offset = (c % 2 * BLOCKS + b) * BANK
                bank = dh[c, b] = dh_banks.tile([P, PACK, P], F32, name=f"dh_{c}_{b}", offset=offset)
                for t in range(PACK):
                    nc.tensor.matmul_mx(
                        out=bank[:, t, :],
                        lhsT=w2_code[e][:, 2 * P * t : 2 * P * (t + 1)].bitcast(E2M1X4),
                        lhsT_scale=w2_scale[:, e, P * t : P * (t + 1)],
                        rhs=g_code[c][:, block].bitcast(E5M2X4),
                        rhs_scale=g_scale[c][:, block],
                        start=True,
                        stop=True,
                    )

        def mask(c):
            if c in (0, CHUNKS - 1):
                for b in range(BLOCKS):
                    offset = masked_bytes(c, b)
                    masked[c, b] = two_places.tile([P, PACK, P], F32, name=f"masked_{c}_{b}", align_bytes=64, offset=offset)[:]
            else:
                offset = masked_bytes(c, 0)
                masked[c] = two_places.tile([P, PACK, CHUNK], F32, name=f"masked_{c}", align_bytes=64, offset=offset)
                for b in range(BLOCKS):
                    masked[c, b] = masked[c][:, :, b * P : (b + 1) * P]
            for b in range(BLOCKS):
                nc.vector.scalar_tensor_tensor(
                    masked[c, b], saved["a1", c][:, :, b * P : (b + 1) * P], 0.0, dh[c, b][:], IS_GT, MULT
                )
                if (c, b) == (0, 0):
                    quantise_g(1)
                    hidden_gradient(1)

        def first_product(engine, c, b):
            block = slice(b * P, (b + 1) * P)
            engine.tensor_tensor(
                to_columns(da[c][:, 0, block]), from_rows(masked[c, b]), from_rows(saved["a3", c][:, :, block]), MULT
            )

        def products(c):
            if c == 0:
                for b in range(BLOCKS):
                    first_product(nc.gpsimd, c, b)
            elif c == CHUNKS - 1:
                first_product(nc.gpsimd, c, 0)
            else:
                nc.gpsimd.tensor_tensor(to_columns(da[c][:, 0]), from_rows(masked[c][:]), from_rows(saved["a3", c]), MULT)
            for b in range(BLOCKS):
                block = slice(b * P, (b + 1) * P)
                nc.vector.scalar_tensor_tensor(
                    da[c][:, 1, block, :],
                    saved["a1", c][:, :, block].rearrange("p t c -> p c t"),
                    0.0,
                    dh[c, b][:].rearrange("p t c -> p c t"),
                    MAX,
                    MULT,
                )
            if c == CHUNKS - 1:
                first_product(nc.vector, c, 1)
                copy_dx(c - 1, 1)

        windows = [held.tile([P, T], F32, name=f"window_{k}") for k in range(K_BLOCKS)]

        dx, dx_bank = {}, {}

        def on_vector(c, k):
            return k == 1 and c >= CHUNKS - 2

        def copy_dx(c, k):
            copy = nc.vector.tensor_copy if on_vector(c, k) else nc.scalar.copy
            copy(dx[c][:, k, :], dx_bank[c, k][:, k, :])

        def scatter(c, k):
            place = windows[k][:].indirect(entries(c * CHUNK, CHUNK))
            if on_vector(c, k):
                nc.vector.tensor_copy(place, dx[c][:, k, :])
            else:
                nc.scalar.activation(place, dx[c][:, k, :], COPY)

        def input_gradient(c):
            e = c * CHUNK // C
            code = ring.tile([P, 2 * CHUNK], U32, name="da_code", align_bytes=64)
            scale = ring.tile([P, 2 * CHUNK], U8, name="da_scale", align_bytes=64)
            quantise(da[c].rearrange("p a c t -> p (a c t)"), code[:], scale[:])
            if c == CHUNKS - 2:
                dx[c] = after_a1.tile([P, K_BLOCKS, CHUNK], F32, name="dx_late", align_bytes=64, offset=0)
            else:
                dx[c] = ring.tile([P, K_BLOCKS, CHUNK], F32, name="dx_out")
            for k in reversed(range(K_BLOCKS)):
                if c in (0, CHUNKS - 1):
                    bank = dh_banks.tile([P, K_BLOCKS, CHUNK], F32, name=f"dx_{c}_{k}", offset=(1 - k) * BANK)
                elif k == K_BLOCKS - 1:
                    bank = dx_banks.tile([P, K_BLOCKS, CHUNK], F32, name="dx")
                dx_bank[c, k] = bank
                for a, (name, w_scale) in enumerate((("w1", w1_scale), ("w3", w3_scale))):
                    nc.tensor.matmul_mx(
                        out=bank[:, k, :],
                        lhsT=w_code[name, e][:, 2 * P * k : 2 * P * (k + 1)].bitcast(E2M1X4),
                        lhsT_scale=w_scale[:, e, P * k : P * (k + 1)],
                        rhs=code[:, a * CHUNK : (a + 1) * CHUNK].bitcast(E5M2X4),
                        rhs_scale=scale[:, a * CHUNK : (a + 1) * CHUNK],
                        start=a == 0,
                        stop=a == 1,
                    )

        def bring_back(c, halves):
            for k in halves:
                copy_dx(c, k)
            for k in halves:
                scatter(c, k)

        permute_w2_scale()
        for j in range(PACK - 1):
            gather_gated(j, 0, GATED)
            gather_ungated(j, GATED, CHUNKS)
        permute_w2(0)
        for c in range(GATED - 1):
            gather_gated(PACK - 1, c, c + 1)
        round_gated(0)
        round_gated(1)
        quantise_g(0)
        hidden_gradient(0)
        gather_gated(PACK - 1, GATED - 1, GATED)
        mask(0)
        gather_ungated(PACK - 1, GATED, GATED + 2)
        round_gated(2)
        permute_w2(1)
        round_gated(3)
        gather_ungated(PACK - 1, GATED + 2, GATED + 3)
        gather_ungated(PACK - 1, GATED + 3, CHUNKS)
        permute_w2(2)
        permute_w2(3)
        blocks = list(range(GATED * BLOCKS, CHUNKS * BLOCKS))
        for c in range(CHUNKS):
            products(c)
            for block in blocks[: (1, 2, 1, 1, 2, 1, 0, 0)[c]]:
                gate_and_round(blocks.pop(0))
            if c + 1 < CHUNKS:
                mask(c + 1)
            if 0 < c < CHUNKS - 2:
                quantise_g(c + 2)
                hidden_gradient(c + 2)
            input_gradient(c)
            if c == CHUNKS - 1:
                scatter(c - 1, 1)
                bring_back(c - 1, (0,))
            if c != CHUNKS - 2:
                bring_back(c, (1, 0))
            if c == 0:
                quantise_g(c + 2)
                hidden_gradient(c + 2)
        for k, queue in enumerate((nc.scalar, nc.sync)):
            queue.dma_start(out[k * P : (k + 1) * P, :], windows[k][:])
